import numpy as np
import ml_dtypes


def mxq(x, axis, fmt="e4m3"):
    dtype, down = {"e4m3": (ml_dtypes.float8_e4m3fn, 7), "e5m2": (ml_dtypes.float8_e5m2, 14)}[fmt]
    v = np.moveaxis(np.asarray(x, np.float32).astype(ml_dtypes.bfloat16).astype(np.float64), axis, -1)
    blocks = v.reshape(v.shape[:-1] + (-1, 32))
    amax = np.abs(blocks).max(-1, keepdims=True)
    byte = np.maximum(np.where(amax > 0, np.frexp(amax)[1] - 1 + 127, 0) - down, 1)
    scale = np.exp2(byte - 127.0)
    codes = (blocks / scale).astype(np.float32).astype(dtype).astype(np.float64)
    return np.moveaxis((codes * scale).reshape(v.shape), -1, axis)


WIDE = False


def mx_kscale(k):
    if not WIDE:
        return np.ones(k)
    levels = np.array([10, -10, 5, -5, 0])
    if k % 512:
        return np.exp2(np.random.permutation(np.resize(levels, k // 32))).repeat(32)
    a = np.empty((k // 512, 16))
    for p in range(k // 512):
        a[p, :8] = np.random.permutation(np.resize(levels, 8))
        for g in range(8):
            far = levels[np.abs(levels - a[p, g]) >= 10]
            a[p, g + 8] = far[np.random.randint(len(far))]
    return np.exp2(a.ravel()).repeat(32)


def f64(x):
    return np.asarray(x).astype(np.float64)


def striped(idx):
    return np.tile(idx.reshape(-1, 16).T, (8, 1)).astype(np.uint16)


def unstriped(offs):
    return offs[:16].T.reshape(-1).astype(np.int64)


def pack_weight(w):
    k, n = w.shape
    w = f64(np.asarray(w, np.float32).astype(ml_dtypes.bfloat16)).reshape(k // 32, 32, n)
    amax = np.abs(w).max(1)
    byte = np.clip(np.where(amax > 0, np.frexp(amax)[1] - 1 + 127 - 7, 1), 1, 254)
    scaled = (w * np.exp2(127.0 - byte)[:, None, :]).reshape(k, n).astype(np.float32)
    words = np.ascontiguousarray(scaled.reshape(k // 512, 128, 4, n).transpose(0, 1, 3, 2)).astype(ml_dtypes.float8_e4m3fn).view(np.uint8)
    return words, np.ascontiguousarray(byte.astype(np.uint8).reshape(k // 512, 16, n))


def unpack_weight(words, scales):
    g, p, n, _ = words.shape
    vals = np.ascontiguousarray(words).view(ml_dtypes.float8_e4m3fn).astype(np.float64) * np.repeat(np.exp2(scales.astype(np.float64) - 127.0), 8, axis=1)[..., None]
    return vals.transpose(0, 1, 3, 2).reshape(g * 512, n)


K, T, S, V, N = 512, 4096, 1536, 768, 256


def setup_inputs():
    n = np.random.standard_normal
    s = mx_kscale(K)[:, None]
    packed_xT = pack_weight(n((K, T)) * s)
    return {
        "x_words": packed_xT[0],
        "x_scales": packed_xT[1],
        "w1": (n((K, N)) / np.sqrt(K) / s).astype(np.float32),
        "w2": (n((K, N)) / np.sqrt(K) / s).astype(np.float32),
        "offs": striped(np.random.permutation(T)[:S]),
    }


def reference(x_words, x_scales, w1, w2, offs):
    xq = unpack_weight(x_words, x_scales)[:, unstriped(offs)]
    e = np.exp(mxq(f64(w1), 0, "e4m3").T @ xq)
    h = mxq(f64(w2), 0, "e4m3").T @ xq
    num = e[:, :V] * h[:, :V] + e[:, V:2 * V] * h[:, V:2 * V]
    den = e[:, :V] + e[:, V:2 * V]
    return num / den

@@ -1,0 +1,194 @@
+from contextlib import ExitStack
+
+import concourse.mybir as mybir
+
+K, T, S, V, N = 512, 4096, 1536, 768, 256
+FLOPS = 2 * 2 * K * N * S
+
+F32 = mybir.dt.float32
+BF16 = mybir.dt.bfloat16
+I32 = mybir.dt.int32
+U32 = mybir.dt.uint32
+U16 = mybir.dt.uint16
+U8 = mybir.dt.uint8
+FP8X4 = mybir.dt.float8_e4m3fn_x4
+ACT = mybir.ActivationFunctionType
+ALU = mybir.AluOpType
+
+P = 128
+PACK = 4
+G = 512
+HEAD = 256
+
+
+def tile_picked_apool_none_p_kernel(tc, x_words, x_scales, w1, w2, offs, out):
+    nc = tc.nc
+    with ExitStack() as ctx:
+        keep = ctx.enter_context(tc.tile_pool(name="keep", bufs=1))
+        psum = ctx.enter_context(tc.psum_pool(name="psum", bufs=1))
+
+        offsets = keep.tile([P, S // 16], U16, name="offsets")
+        nc.sync.dma_start(offsets[:], offs)
+
+        w1_raw = keep.tile([P, PACK, N], F32, name="w1_raw")
+        nc.sync.dma_start(out=w1_raw[:], in_=w1.rearrange("(p j) n -> p j n", j=PACK))
+
+        scale_table = keep.tile([P, T], U8, name="scale_table", align_bytes=64)
+        nc.vector.memset(scale_table[:].bitcast(I32), 0)
+        for q in (0, 2, 1, 3):
+            nc.sync.dma_start(
+                out=scale_table[32 * q : 32 * q + 4, :].bitcast(I32),
+                in_=x_scales[0][4 * q : 4 * q + 4, :].bitcast(I32),
+            )
+
+        word_table = keep.tile([P, T], I32, name="word_table", align_bytes=64)
+        nc.sync.dma_start(out=word_table[:], in_=x_words[0].rearrange("p n t -> p (n t)").bitcast(I32))
+
+        w2_raw = keep.tile([P, PACK, N], F32, name="w2_raw")
+        nc.sync.dma_start(out=w2_raw[:], in_=w2.rearrange("(p j) n -> p j n", j=PACK))
+
+        def cast(dst, src, sign):
+            nc.scalar.activation(
+                out=dst.rearrange("p (c i t) -> p c t i", i=4, t=PACK),
+                in_=src.rearrange("p t (c i) -> p c t i", i=4),
+                func=ACT.Copy,
+                scale=sign,
+            )
+
+        def stage(name, raw, c0, width, factor):
+            staged = keep.tile([P, 2, width * PACK], BF16, name=name, align_bytes=64)
+            cast(staged[:, 0, :], raw[:, :, c0 : c0 + width], factor)
+            cast(staged[:, 1, :], raw[:, :, c0 : c0 + width], -factor)
+            return staged
+
+        def quantise(name, staged, width, tag):
+            codes = keep.tile([P, 2 * width], U32, name=name + "_codes", tag=tag, align_bytes=64)
+            scales = keep.tile([P, 2 * width], U8, name=name + "_scales", align_bytes=64)
+            nc.vector.quantize_mx(
+                out=codes[:].bitcast(FP8X4), scales=scales[:], in_=staged[:].rearrange("p s c -> p (s c)")
+            )
+            return codes, scales
+
+        picked_scales = keep.tile([P, S], U8, name="picked_scales", align_bytes=64)
+        nc.vector.tensor_copy(picked_scales[:], scale_table[:].indirect(offsets[:]))
+
+        w1_staged = stage("w1_staged", w1_raw, 0, N, 1.0)
+        w1q = quantise("w1", w1_staged, N, "scale_table")
+
+        def gather_words(dst, e0):
+            nc.vector.tensor_copy(
+                dst, word_table[:].bitcast(U32).indirect(offsets[:, e0 // 16 : (e0 + G) // 16])
+            )
+
+        early = keep.tile([P, 2 * G], U32, name="early", align_bytes=64)
+
+        def mm(acc, weights, c0, words, w0, e0, width, start, stop):
+            nc.tensor.matmul_mx(
+                out=acc,
+                lhsT=weights[0][:, c0 : c0 + P].bitcast(FP8X4),
+                lhsT_scale=weights[1][:, c0 : c0 + P],
+                rhs=words[:, w0 : w0 + width].bitcast(FP8X4),
+                rhs_scale=picked_scales[:, e0 : e0 + width],
+                start=start,
+                stop=stop,
+            )
+
+        def bank(name, tag):
+            return psum.tile([P, G], F32, name=name, tag=tag)
+
+        warm = bank("warm", "b7")
+        for rep in range(4):
+            nc.tensor.matmul_mx(
+                out=warm[0:32, :],
+                lhsT=w1q[0][:, 0:32].bitcast(FP8X4),
+                lhsT_scale=w1q[1][:, 0:32],
+                rhs=w1q[0][:].bitcast(FP8X4),
+                rhs_scale=w1q[1][:],
+                start=True,
+                stop=True,
+            )
+
+        gather_words(early[:, 0:G], 0)
+        d_head = [bank("d_head%d" % m, "b%d" % m) for m in range(2)]
+        for m in range(2):
+            mm(d_head[m][:, 0:HEAD], w1q, N + m * P, early, 0, 0, HEAD, True, False)
+
+        gather_words(early[:, G : 2 * G], G)
+        for m in range(2):
+            mm(d_head[m][:, 0:HEAD], w1q, m * P, early, V, V, HEAD, False, True)
+        d_tail = [bank("d_tail%d" % m, "b%d" % (2 + m)) for m in range(2)]
+        for m in range(2):
+            mm(d_tail[m][:], w1q, N + m * P, early, HEAD, HEAD, G, True, False)
+
+        w2_staged = [stage("w2_staged%d" % m, w2_raw, m * P, P, 0.5) for m in range(2)]
+        w2q = [None, None]
+        w2q[0] = quantise("w2a", w2_staged[0], P, "w2a_codes")
+
+        gates = keep.tile([P, 2 * V], F32, name="gates", tag="w2_raw")
+        gate = [gates[:, m * V : (m + 1) * V] for m in range(2)]
+        prod = [keep.tile([P, V], F32, name="prod%d" % m) for m in range(2)]
+        other = [keep.tile([P, HEAD], F32, name="other%d" % m) for m in range(2)]
+        res = [keep.tile([P, V], F32, name="res%d" % m) for m in range(2)]
+
+        def head_products(m, tag):
+            y = bank("head%d" % m, tag)
+            mm(y[:, 0:HEAD], w2q[m], 0, early, V, V, HEAD, True, True)
+            mm(y[:, HEAD:G], w2q[m], 0, early, 0, 0, HEAD, True, True)
+            return y
+
+        def tanh_half(dst, src):
+            nc.scalar.activation(out=dst, in_=src, func=ACT.Tanh, scale=0.5)
+
+        def weigh(dst, m, c0, c1, shift, values):
+            nc.vector.scalar_tensor_tensor(
+                out=dst, in0=gate[m][:, c0:c1], scalar=shift, in1=values, op0=ALU.add, op1=ALU.mult
+            )
+
+        def blend(m, c0, c1, base):
+            nc.vector.scalar_tensor_tensor(
+                out=res[m][:, c0:c1], in0=base, scalar=2.0, in1=prod[m][:, c0:c1], op0=ALU.mult, op1=ALU.add
+            )
+
+        def join(m):
+            nc.gpsimd.tensor_tensor(out=res[m][:, 0:HEAD], in0=prod[m][:, 0:HEAD], in1=other[m][:], op=ALU.subtract)
+
+        head0 = head_products(0, "b4")
+        diff0 = bank("diff0", "b5")
+        base0 = bank("base0", "b6")
+        mm(diff0[:], w2q[0], P, early, HEAD, HEAD, G, True, False)
+
+        late = keep.tile([P, G], U32, name="late", tag="w2_staged0", align_bytes=64)
+        gather_words(late[:], 2 * G)
+        w2q[1] = quantise("w2b", w2_staged[1], P, "w2b_codes")
+
+        for m in range(2):
+            tanh_half(gate[m][:, 0:HEAD], d_head[m][:, 0:HEAD])
+        mm(d_tail[0][:], w1q, 0, late, 0, 2 * G, G, False, True)
+        mm(diff0[:], w2q[0], 0, late, 0, 2 * G, G, False, True)
+        mm(d_tail[1][:], w1q, P, late, 0, 2 * G, G, False, True)
+        mm(base0[:], w2q[0], 0, early, HEAD, HEAD, G, True, True)
+        for m in range(2):
+            tanh_half(gate[m][:, HEAD:V], d_tail[m][:])
+
+        head1 = head_products(1, "b7")
+        diff1 = bank("diff1", "b0")
+        base1 = bank("base1", "b1")
+        mm(diff1[:], w2q[1], P, early, HEAD, HEAD, G, True, False)
+        mm(diff1[:], w2q[1], 0, late, 0, 2 * G, G, False, True)
+        mm(base1[:], w2q[1], 0, early, HEAD, HEAD, G, True, True)
+
+        weigh(prod[0][:, 0:HEAD], 0, 0, HEAD, 1.0, head0[:, 0:HEAD])
+        weigh(other[0][:], 0, 0, HEAD, -1.0, head0[:, HEAD:G])
+        join(0)
+        weigh(prod[0][:, HEAD:V], 0, HEAD, V, 1.0, diff0[:])
+        weigh(prod[1][:, 0:HEAD], 1, 0, HEAD, 1.0, head1[:, 0:HEAD])
+        blend(0, HEAD, V, base0[:])
+        nc.sync.dma_start(out=out[0:P, :], in_=res[0][:])
+        weigh(other[1][:], 1, 0, HEAD, -1.0, head1[:, HEAD:G])
+        join(1)
+        nc.sync.dma_start(out=out[P : 2 * P, 0:HEAD], in_=res[1][:, 0:HEAD])
+        for c0 in (HEAD, G):
+            weigh(prod[1][:, c0 : c0 + HEAD], 1, c0, c0 + HEAD, 1.0, diff1[:, c0 - HEAD : c0])
+        for c0 in (HEAD, G):
+            blend(1, c0, c0 + HEAD, base1[:, c0 - HEAD : c0])
+            nc.sync.dma_start(out=out[P : 2 * P, c0 : c0 + HEAD], in_=res[1][:, c0 : c0 + HEAD])

@@ -19,6 +19,7 @@ P = 128
 PACK = 4
 G = 512
 HEAD = 256
+WARM = 5
 
 
 def tile_picked_apool_none_p_kernel(tc, x_words, x_scales, w1, w2, offs, out):
@@ -35,11 +36,7 @@ def tile_picked_apool_none_p_kernel(tc, x_words, x_scales, w1, w2, offs, out):
 
         scale_table = keep.tile([P, T], U8, name="scale_table", align_bytes=64)
         nc.vector.memset(scale_table[:].bitcast(I32), 0)
-        for q in (0, 2, 1, 3):
-            nc.sync.dma_start(
-                out=scale_table[32 * q : 32 * q + 4, :].bitcast(I32),
-                in_=x_scales[0][4 * q : 4 * q + 4, :].bitcast(I32),
-            )
+        nc.sync.dma_start(out=scale_table[4:P:8, :].bitcast(I32), in_=x_scales[0].bitcast(I32))
 
         word_table = keep.tile([P, T], I32, name="word_table", align_bytes=64)
         nc.sync.dma_start(out=word_table[:], in_=x_words[0].rearrange("p n t -> p (n t)").bitcast(I32))
@@ -47,33 +44,35 @@ def tile_picked_apool_none_p_kernel(tc, x_words, x_scales, w1, w2, offs, out):
         w2_raw = keep.tile([P, PACK, N], F32, name="w2_raw")
         nc.sync.dma_start(out=w2_raw[:], in_=w2.rearrange("(p j) n -> p j n", j=PACK))
 
-        def cast(dst, src, sign):
+        def cast(dst, src, factor):
             nc.scalar.activation(
                 out=dst.rearrange("p (c i t) -> p c t i", i=4, t=PACK),
                 in_=src.rearrange("p t (c i) -> p c t i", i=4),
                 func=ACT.Copy,
-                scale=sign,
+                scale=factor,
             )
-
-        def stage(name, raw, c0, width, factor):
-            staged = keep.tile([P, 2, width * PACK], BF16, name=name, align_bytes=64)
-            cast(staged[:, 0, :], raw[:, :, c0 : c0 + width], factor)
-            cast(staged[:, 1, :], raw[:, :, c0 : c0 + width], -factor)
-            return staged
 
         def quantise(name, staged, width, tag):
-            codes = keep.tile([P, 2 * width], U32, name=name + "_codes", tag=tag, align_bytes=64)
-            scales = keep.tile([P, 2 * width], U8, name=name + "_scales", align_bytes=64)
-            nc.vector.quantize_mx(
-                out=codes[:].bitcast(FP8X4), scales=scales[:], in_=staged[:].rearrange("p s c -> p (s c)")
-            )
+            codes = keep.tile([P, width], U32, name=name + "_codes", tag=tag, align_bytes=64)
+            scales = keep.tile([P, width], U8, name=name + "_scales", align_bytes=64)
+            nc.vector.quantize_mx(out=codes[:].bitcast(FP8X4), scales=scales[:], in_=staged[:])
             return codes, scales
 
         picked_scales = keep.tile([P, S], U8, name="picked_scales", align_bytes=64)
-        nc.vector.tensor_copy(picked_scales[:], scale_table[:].indirect(offsets[:]))
+        nc.vector.memset(picked_scales[:].bitcast(I32), 0)
+        spread_scales = keep.tile([P, S], U8, name="spread_scales", align_bytes=64)
+        nc.vector.tensor_copy(spread_scales[:], scale_table[:].indirect(offsets[:]))
 
-        w1_staged = stage("w1_staged", w1_raw, 0, N, 1.0)
-        w1q = quantise("w1", w1_staged, N, "scale_table")
+        w1_staged = keep.tile([P, 2 * N * PACK], BF16, name="w1_staged", align_bytes=64)
+        cast(w1_staged[:, 0 : N * PACK], w1_raw[:], 1.0)
+        cast(w1_staged[:, N * PACK : 2 * N * PACK], w1_raw[:], -1.0)
+        w1q = quantise("w1", w1_staged, 2 * N, "scale_table")
+
+        for q in (0, 2, 1, 3):
+            nc.scalar.dma_start(
+                out=picked_scales[32 * q : 32 * q + 4, :].bitcast(I32),
+                in_=spread_scales[32 * q + 4 : 32 * q + 32 : 8, :].bitcast(I32),
+            )
 
         def gather_words(dst, e0):
             nc.vector.tensor_copy(
@@ -97,7 +96,7 @@ def tile_picked_apool_none_p_kernel(tc, x_words, x_scales, w1, w2, offs, out):
             return psum.tile([P, G], F32, name=name, tag=tag)
 
         warm = bank("warm", "b7")
-        for rep in range(4):
+        for rep in range(WARM):
             nc.tensor.matmul_mx(
                 out=warm[0:32, :],
                 lhsT=w1q[0][:, 0:32].bitcast(FP8X4),
@@ -120,75 +119,65 @@ def tile_picked_apool_none_p_kernel(tc, x_words, x_scales, w1, w2, offs, out):
         for m in range(2):
             mm(d_tail[m][:], w1q, N + m * P, early, HEAD, HEAD, G, True, False)
 
-        w2_staged = [stage("w2_staged%d" % m, w2_raw, m * P, P, 0.5) for m in range(2)]
-        w2q = [None, None]
-        w2q[0] = quantise("w2a", w2_staged[0], P, "w2a_codes")
+        w2_staged = keep.tile([P, N * PACK], BF16, name="w2_staged", align_bytes=64)
+        cast(w2_staged[:], w2_raw[:], 0.5)
+        w2q = quantise("w2", w2_staged, N, "w2_codes")
 
-        gates = keep.tile([P, 2 * V], F32, name="gates", tag="w2_raw")
-        gate = [gates[:, m * V : (m + 1) * V] for m in range(2)]
-        prod = [keep.tile([P, V], F32, name="prod%d" % m) for m in range(2)]
-        other = [keep.tile([P, HEAD], F32, name="other%d" % m) for m in range(2)]
-        res = [keep.tile([P, V], F32, name="res%d" % m) for m in range(2)]
-
-        def head_products(m, tag):
-            y = bank("head%d" % m, tag)
-            mm(y[:, 0:HEAD], w2q[m], 0, early, V, V, HEAD, True, True)
-            mm(y[:, HEAD:G], w2q[m], 0, early, 0, 0, HEAD, True, True)
-            return y
+        gate = keep.tile([P, 2 * V], F32, name="gate", tag="w2_raw")
+        second = keep.tile([P, 2 * V], F32, name="second")
+        first = keep.tile([P, 2 * V], F32, name="first")
+        res = keep.tile([P, 2 * V], F32, name="res")
 
         def tanh_half(dst, src):
             nc.scalar.activation(out=dst, in_=src, func=ACT.Tanh, scale=0.5)
 
-        def weigh(dst, m, c0, c1, shift, values):
+        def weigh(dst, c0, c1, shift, values):
             nc.vector.scalar_tensor_tensor(
-                out=dst, in0=gate[m][:, c0:c1], scalar=shift, in1=values, op0=ALU.add, op1=ALU.mult
+                out=dst[:, c0:c1], in0=gate[:, c0:c1], scalar=shift, in1=values, op0=ALU.add, op1=ALU.mult
             )
 
-        def blend(m, c0, c1, base):
-            nc.vector.scalar_tensor_tensor(
-                out=res[m][:, c0:c1], in0=base, scalar=2.0, in1=prod[m][:, c0:c1], op0=ALU.mult, op1=ALU.add
-            )
+        def join(engine, c0, c1):
+            engine.tensor_tensor(out=res[:, c0:c1], in0=second[:, c0:c1], in1=first[:, c0:c1], op=ALU.subtract)
 
-        def join(m):
-            nc.gpsimd.tensor_tensor(out=res[m][:, 0:HEAD], in0=prod[m][:, 0:HEAD], in1=other[m][:], op=ALU.subtract)
+        head_first = bank("head_first", "b4")
+        head_second = bank("head_second", "b5")
+        for m in range(2):
+            mm(head_first[:, m * HEAD : (m + 1) * HEAD], w2q, m * P, early, 0, 0, HEAD, True, True)
+        for m in range(2):
+            mm(head_second[:, m * HEAD : (m + 1) * HEAD], w2q, m * P, early, V, V, HEAD, True, True)
 
-        head0 = head_products(0, "b4")
-        diff0 = bank("diff0", "b5")
-        base0 = bank("base0", "b6")
-        mm(diff0[:], w2q[0], P, early, HEAD, HEAD, G, True, False)
-
-        late = keep.tile([P, G], U32, name="late", tag="w2_staged0", align_bytes=64)
+        late = keep.tile([P, G], U32, name="late", tag="w2_staged", align_bytes=64)
         gather_words(late[:], 2 * G)
-        w2q[1] = quantise("w2b", w2_staged[1], P, "w2b_codes")
 
         for m in range(2):
-            tanh_half(gate[m][:, 0:HEAD], d_head[m][:, 0:HEAD])
-        mm(d_tail[0][:], w1q, 0, late, 0, 2 * G, G, False, True)
-        mm(diff0[:], w2q[0], 0, late, 0, 2 * G, G, False, True)
-        mm(d_tail[1][:], w1q, P, late, 0, 2 * G, G, False, True)
-        mm(base0[:], w2q[0], 0, early, HEAD, HEAD, G, True, True)
+            tanh_half(gate[:, m * HEAD : (m + 1) * HEAD], d_head[m][:, 0:HEAD])
+        tail_first = [bank("tail_first%d" % m, "b%d" % (6 + m)) for m in range(2)]
+        tail_second = [bank("tail_second%d" % m, "b%d" % m) for m in range(2)]
         for m in range(2):
-            tanh_half(gate[m][:, HEAD:V], d_tail[m][:])
+            mm(d_tail[m][:], w1q, m * P, late, 0, 2 * G, G, False, True)
+            tanh_half(gate[:, (m + 1) * G : (m + 2) * G], d_tail[m][:])
+        for m in range(2):
+            mm(tail_first[m][:], w2q, m * P, early, HEAD, HEAD, G, True, True)
+            mm(tail_second[m][:], w2q, m * P, late, 0, 2 * G, G, True, True)
 
-        head1 = head_products(1, "b7")
-        diff1 = bank("diff1", "b0")
-        base1 = bank("base1", "b1")
-        mm(diff1[:], w2q[1], P, early, HEAD, HEAD, G, True, False)
-        mm(diff1[:], w2q[1], 0, late, 0, 2 * G, G, False, True)
-        mm(base1[:], w2q[1], 0, early, HEAD, HEAD, G, True, True)
+        weigh(first, 0, G, -1.0, head_first[:])
+        weigh(second, 0, G, 1.0, head_second[:])
+        join(nc.gpsimd, 0, G)
+        nc.sync.dma_start(
+            out=out[:, 0:HEAD].rearrange("(m p) v -> p m v", p=P),
+            in_=res[:, 0:G].rearrange("p (m v) -> p m v", m=2),
+        )
 
-        weigh(prod[0][:, 0:HEAD], 0, 0, HEAD, 1.0, head0[:, 0:HEAD])
-        weigh(other[0][:], 0, 0, HEAD, -1.0, head0[:, HEAD:G])
-        join(0)
-        weigh(prod[0][:, HEAD:V], 0, HEAD, V, 1.0, diff0[:])
-        weigh(prod[1][:, 0:HEAD], 1, 0, HEAD, 1.0, head1[:, 0:HEAD])
-        blend(0, HEAD, V, base0[:])
-        nc.sync.dma_start(out=out[0:P, :], in_=res[0][:])
-        weigh(other[1][:], 1, 0, HEAD, -1.0, head1[:, HEAD:G])
-        join(1)
-        nc.sync.dma_start(out=out[P : 2 * P, 0:HEAD], in_=res[1][:, 0:HEAD])
-        for c0 in (HEAD, G):
-            weigh(prod[1][:, c0 : c0 + HEAD], 1, c0, c0 + HEAD, 1.0, diff1[:, c0 - HEAD : c0])
-        for c0 in (HEAD, G):
-            blend(1, c0, c0 + HEAD, base1[:, c0 - HEAD : c0])
-            nc.sync.dma_start(out=out[P : 2 * P, c0 : c0 + HEAD], in_=res[1][:, c0 : c0 + HEAD])
+        weigh(first, G, 2 * G, -1.0, tail_first[0][:])
+        weigh(second, G, 2 * G, 1.0, tail_second[0][:])
+        join(nc.gpsimd, G, 2 * G)
+        nc.sync.dma_start(out=out[0:P, HEAD:V], in_=res[:, G : 2 * G])
+
+        weigh(first, 2 * G, 3 * G, -1.0, tail_first[1][:])
+        for c0 in (0, HEAD):
+            weigh(second, 2 * G + c0, 2 * G + c0 + HEAD, 1.0, tail_second[1][:, c0 : c0 + HEAD])
+        for c0 in (0, HEAD):
+            join(nc.vector, 2 * G + c0, 2 * G + c0 + HEAD)
+            nc.sync.dma_start(
+                out=out[P : 2 * P, HEAD + c0 : 2 * HEAD + c0], in_=res[:, 2 * G + c0 : 2 * G + c0 + HEAD]
+            )

@@ -19,13 +19,14 @@ P = 128
 PACK = 4
 G = 512
 HEAD = 256
-WARM = 5
+WARM = 3
 
 
 def tile_picked_apool_none_p_kernel(tc, x_words, x_scales, w1, w2, offs, out):
     nc = tc.nc
     with ExitStack() as ctx:
         keep = ctx.enter_context(tc.tile_pool(name="keep", bufs=1))
+        shared = ctx.enter_context(tc.tile_pool(name="shared", bufs=1))
         psum = ctx.enter_context(tc.psum_pool(name="psum", bufs=1))
 
         offsets = keep.tile([P, S // 16], U16, name="offsets")
@@ -119,13 +120,16 @@ def tile_picked_apool_none_p_kernel(tc, x_words, x_scales, w1, w2, offs, out):
         for m in range(2):
             mm(d_tail[m][:], w1q, N + m * P, early, HEAD, HEAD, G, True, False)
 
-        w2_staged = keep.tile([P, N * PACK], BF16, name="w2_staged", align_bytes=64)
+        w2_staged = shared.tile([P, N * PACK], BF16, name="w2_staged", align_bytes=64, offset=1024)
         cast(w2_staged[:], w2_raw[:], 0.5)
         w2q = quantise("w2", w2_staged, N, "w2_codes")
+        w2n_staged = [keep.tile([P, P * PACK], BF16, name="w2n_staged%d" % m, align_bytes=64) for m in range(2)]
+        cast(w2n_staged[0][:], w2_raw[:, :, 0:P], -0.5)
 
-        gate = keep.tile([P, 2 * V], F32, name="gate", tag="w2_raw")
+        gate_head = shared.tile([P, G], F32, name="gate_head", align_bytes=64, offset=2048)
+        gate_tail = keep.tile([P, 2 * G], F32, name="gate_tail")
         second = keep.tile([P, 2 * V], F32, name="second")
-        first = keep.tile([P, 2 * V], F32, name="first")
+        first = keep.tile([P, G], F32, name="first")
         res = keep.tile([P, 2 * V], F32, name="res")
 
         def tanh_half(dst, src):
@@ -133,7 +137,7 @@ def tile_picked_apool_none_p_kernel(tc, x_words, x_scales, w1, w2, offs, out):
 
         def weigh(dst, c0, c1, shift, values):
             nc.vector.scalar_tensor_tensor(
-                out=dst[:, c0:c1], in0=gate[:, c0:c1], scalar=shift, in1=values, op0=ALU.add, op1=ALU.mult
+                out=dst[:, c0:c1], in0=(gate_head[:, c0:c1] if c1 <= G else gate_tail[:, c0 - G : c1 - G]), scalar=shift, in1=values, op0=ALU.add, op1=ALU.mult
             )
 
         def join(engine, c0, c1):
@@ -146,38 +150,45 @@ def tile_picked_apool_none_p_kernel(tc, x_words, x_scales, w1, w2, offs, out):
         for m in range(2):
             mm(head_second[:, m * HEAD : (m + 1) * HEAD], w2q, m * P, early, V, V, HEAD, True, True)
 
-        late = keep.tile([P, G], U32, name="late", tag="w2_staged", align_bytes=64)
-        gather_words(late[:], 2 * G)
+        base = [bank("base%d" % m, "b%d" % (6 + m)) for m in range(2)]
 
         for m in range(2):
-            tanh_half(gate[:, m * HEAD : (m + 1) * HEAD], d_head[m][:, 0:HEAD])
-        tail_first = [bank("tail_first%d" % m, "b%d" % (6 + m)) for m in range(2)]
-        tail_second = [bank("tail_second%d" % m, "b%d" % m) for m in range(2)]
+            tanh_half(gate_head[:, m * HEAD : (m + 1) * HEAD], d_head[m][:, 0:HEAD])
+        cast(w2n_staged[1][:], w2_raw[:, :, P : 2 * P], -0.5)
+
+        late = shared.tile([P, G], U32, name="late", align_bytes=64, offset=0)
+        gather_words(late[:], 2 * G)
+        w2nq = [quantise("w2n0", w2n_staged[0], P, "word_table")]
+        weigh(first, 0, G, -1.0, head_first[:])
+        w2nq.append(quantise("w2n1", w2n_staged[1], P, "w2n1_codes"))
+        weigh(second, 0, G, 1.0, head_second[:])
         for m in range(2):
             mm(d_tail[m][:], w1q, m * P, late, 0, 2 * G, G, False, True)
-            tanh_half(gate[:, (m + 1) * G : (m + 2) * G], d_tail[m][:])
+            tanh_half(gate_tail[:, m * G : (m + 1) * G], d_tail[m][:])
+        diff = [bank("diff%d" % m, "b%d" % m) for m in range(2)]
         for m in range(2):
-            mm(tail_first[m][:], w2q, m * P, early, HEAD, HEAD, G, True, True)
-            mm(tail_second[m][:], w2q, m * P, late, 0, 2 * G, G, True, True)
+            mm(diff[m][:], w2q, m * P, late, 0, 2 * G, G, True, False)
+            mm(diff[m][:], w2nq[m], 0, early, HEAD, HEAD, G, False, True)
+            mm(base[m][:], w2q, m * P, early, HEAD, HEAD, G, True, True)
 
-        weigh(first, 0, G, -1.0, head_first[:])
-        weigh(second, 0, G, 1.0, head_second[:])
+        def blend(c0, c1, values):
+            nc.vector.scalar_tensor_tensor(
+                out=res[:, c0:c1], in0=values, scalar=2.0, in1=second[:, c0:c1], op0=ALU.mult, op1=ALU.add
+            )
+
         join(nc.gpsimd, 0, G)
         nc.sync.dma_start(
             out=out[:, 0:HEAD].rearrange("(m p) v -> p m v", p=P),
             in_=res[:, 0:G].rearrange("p (m v) -> p m v", m=2),
         )
 
-        weigh(first, G, 2 * G, -1.0, tail_first[0][:])
-        weigh(second, G, 2 * G, 1.0, tail_second[0][:])
-        join(nc.gpsimd, G, 2 * G)
+        weigh(second, G, 2 * G, 1.0, diff[0][:])
+        weigh(second, 2 * G, 2 * G + HEAD, 1.0, diff[1][:, 0:HEAD])
+        blend(G, 2 * G, base[0][:])
         nc.sync.dma_start(out=out[0:P, HEAD:V], in_=res[:, G : 2 * G])
-
-        weigh(first, 2 * G, 3 * G, -1.0, tail_first[1][:])
+        weigh(second, 2 * G + HEAD, 3 * G, 1.0, diff[1][:, HEAD:G])
         for c0 in (0, HEAD):
-            weigh(second, 2 * G + c0, 2 * G + c0 + HEAD, 1.0, tail_second[1][:, c0 : c0 + HEAD])
-        for c0 in (0, HEAD):
-            join(nc.vector, 2 * G + c0, 2 * G + c0 + HEAD)
+            blend(2 * G + c0, 2 * G + c0 + HEAD, base[1][:, c0 : c0 + HEAD])
             nc.sync.dma_start(
                 out=out[P : 2 * P, HEAD + c0 : 2 * HEAD + c0], in_=res[:, 2 * G + c0 : 2 * G + c0 + HEAD]
             )

@@ -18,7 +18,7 @@ ALU = mybir.AluOpType
 P = 128
 PACK = 4
 G = 512
-HEAD = 256
+W = 256
 WARM = 3
 
 
@@ -26,77 +26,113 @@ def tile_picked_apool_none_p_kernel(tc, x_words, x_scales, w1, w2, offs, out):
     nc = tc.nc
     with ExitStack() as ctx:
         keep = ctx.enter_context(tc.tile_pool(name="keep", bufs=1))
-        shared = ctx.enter_context(tc.tile_pool(name="shared", bufs=1))
         psum = ctx.enter_context(tc.psum_pool(name="psum", bufs=1))
 
         offsets = keep.tile([P, S // 16], U16, name="offsets")
         nc.sync.dma_start(offsets[:], offs)
 
-        w1_raw = keep.tile([P, PACK, N], F32, name="w1_raw")
-        nc.sync.dma_start(out=w1_raw[:], in_=w1.rearrange("(p j) n -> p j n", j=PACK))
+        def load_weights(name, w):
+            raw = keep.tile([P, PACK, N], F32, name=name + "_raw")
+            nc.sync.dma_start(out=raw[:], in_=w.rearrange("(p j) n -> p j n", j=PACK))
+            return raw
 
+        w1_raw = load_weights("w1", w1)
         scale_table = keep.tile([P, T], U8, name="scale_table", align_bytes=64)
         nc.vector.memset(scale_table[:].bitcast(I32), 0)
-        nc.sync.dma_start(out=scale_table[4:P:8, :].bitcast(I32), in_=x_scales[0].bitcast(I32))
+        nc.sync.dma_start(out=scale_table[32:96:4, :].bitcast(I32), in_=x_scales[0].bitcast(I32))
+        w2_raw = load_weights("w2", w2)
 
         word_table = keep.tile([P, T], I32, name="word_table", align_bytes=64)
         nc.sync.dma_start(out=word_table[:], in_=x_words[0].rearrange("p n t -> p (n t)").bitcast(I32))
 
-        w2_raw = keep.tile([P, PACK, N], F32, name="w2_raw")
-        nc.sync.dma_start(out=w2_raw[:], in_=w2.rearrange("(p j) n -> p j n", j=PACK))
-
-        def cast(dst, src, factor):
-            nc.scalar.activation(
-                out=dst.rearrange("p (c i t) -> p c t i", i=4, t=PACK),
-                in_=src.rearrange("p t (c i) -> p c t i", i=4),
-                func=ACT.Copy,
-                scale=factor,
+        picked_scales = keep.tile([P, S], U8, name="picked_scales", align_bytes=64)
+        nc.gpsimd.memset(picked_scales[:].bitcast(I32), 0)
+        spread_scales = keep.tile([P, S], U8, name="spread_scales", align_bytes=64)
+        nc.vector.tensor_copy(spread_scales[:], scale_table[:].indirect(offsets[:]))
+        for q in (0, 2, 1, 3):
+            nc.sync.dma_start(
+                out=picked_scales[32 * q : 32 * q + 4, :].bitcast(I32),
+                in_=spread_scales[32 + 16 * q : 48 + 16 * q : 4, :].bitcast(I32),
             )
 
-        def quantise(name, staged, width, tag):
-            codes = keep.tile([P, width], U32, name=name + "_codes", tag=tag, align_bytes=64)
-            scales = keep.tile([P, width], U8, name=name + "_scales", align_bytes=64)
+        def quantise(name, raw, factor, negate_on_vector):
+            staged = keep.tile([P, 2 * N * PACK], BF16, name=name + "_staged", align_bytes=64)
+            rows = raw[:].rearrange("p t (c i) -> p c t i", i=4)
+            plus, minus = (
+                staged[:, h * N * PACK : (h + 1) * N * PACK].rearrange("p (c i t) -> p c t i", i=4, t=PACK)
+                for h in range(2)
+            )
+            nc.scalar.activation(out=plus, in_=rows, func=ACT.Copy, scale=factor)
+            if negate_on_vector:
+                nc.vector.tensor_scalar(out=minus, in0=rows, scalar1=-factor, scalar2=None, op0=ALU.mult)
+            else:
+                nc.scalar.activation(out=minus, in_=rows, func=ACT.Copy, scale=-factor)
+            codes = keep.tile([P, 2 * N], U32, name=name + "_codes", align_bytes=64)
+            scales = keep.tile([P, 2 * N], U8, name=name + "_scales", align_bytes=64)
             nc.vector.quantize_mx(out=codes[:].bitcast(FP8X4), scales=scales[:], in_=staged[:])
             return codes, scales
 
-        picked_scales = keep.tile([P, S], U8, name="picked_scales", align_bytes=64)
-        nc.vector.memset(picked_scales[:].bitcast(I32), 0)
-        spread_scales = keep.tile([P, S], U8, name="spread_scales", align_bytes=64)
-        nc.vector.tensor_copy(spread_scales[:], scale_table[:].indirect(offsets[:]))
+        w1q = quantise("w1", w1_raw, 1.0, False)
+        w2q = quantise("w2", w2_raw, 0.5, True)
 
-        w1_staged = keep.tile([P, 2 * N * PACK], BF16, name="w1_staged", align_bytes=64)
-        cast(w1_staged[:, 0 : N * PACK], w1_raw[:], 1.0)
-        cast(w1_staged[:, N * PACK : 2 * N * PACK], w1_raw[:], -1.0)
-        w1q = quantise("w1", w1_staged, 2 * N, "scale_table")
-
-        for q in (0, 2, 1, 3):
-            nc.scalar.dma_start(
-                out=picked_scales[32 * q : 32 * q + 4, :].bitcast(I32),
-                in_=spread_scales[32 * q + 4 : 32 * q + 32 : 8, :].bitcast(I32),
-            )
+        early = keep.tile([P, 2 * G], U32, name="early", align_bytes=64)
+        late = keep.tile([P, G], U32, name="late", align_bytes=64)
 
         def gather_words(dst, e0):
             nc.vector.tensor_copy(
                 dst, word_table[:].bitcast(U32).indirect(offsets[:, e0 // 16 : (e0 + G) // 16])
             )
 
-        early = keep.tile([P, 2 * G], U32, name="early", align_bytes=64)
-
-        def mm(acc, weights, c0, words, w0, e0, width, start, stop):
+        def mm(acc, weights, m, negated, e0, width, start, stop):
+            c0 = m * P + (N if negated else 0)
+            words = early[:, e0 : e0 + width] if e0 < 2 * G else late[:, e0 - 2 * G : e0 - 2 * G + width]
             nc.tensor.matmul_mx(
                 out=acc,
                 lhsT=weights[0][:, c0 : c0 + P].bitcast(FP8X4),
                 lhsT_scale=weights[1][:, c0 : c0 + P],
-                rhs=words[:, w0 : w0 + width].bitcast(FP8X4),
+                rhs=words.bitcast(FP8X4),
                 rhs_scale=picked_scales[:, e0 : e0 + width],
                 start=start,
                 stop=stop,
             )
 
-        def bank(name, tag):
-            return psum.tile([P, G], F32, name=name, tag=tag)
+        def bank(name, tag=None):
+            return psum.tile([P, G], F32, name=name, tag=tag or name)
 
-        warm = bank("warm", "b7")
+        def half(tile, h):
+            return tile[:, h * W : (h + 1) * W]
+
+        d_head, first_head = bank("d_head"), bank("first_head")
+        d_tail = [bank("d_tail0"), bank("d_tail1")]
+        f_tail = [bank("f_tail0"), bank("f_tail1")]
+        base0 = bank("base0")
+
+        gate = keep.tile([P, 6 * W], F32, name="gate")
+        prod = keep.tile([P, 6 * W], F32, name="prod")
+        res = keep.tile([P, 6 * W], F32, name="res")
+        held = keep.tile([P, 3 * W], F32, name="held")
+
+        def tanh_half(piece, src):
+            nc.scalar.activation(out=half(gate, piece), in_=src, func=ACT.Tanh, scale=-0.5)
+
+        def weigh(dst, piece, shift, src):
+            nc.vector.scalar_tensor_tensor(
+                out=half(dst, piece), in0=half(gate, piece), scalar=shift, in1=src, op0=ALU.add, op1=ALU.mult
+            )
+
+        def join_held(piece):
+            nc.gpsimd.tensor_tensor(out=half(res, piece), in0=half(held, piece), in1=half(prod, piece), op=ALU.subtract)
+
+        def join_base(piece, src):
+            nc.vector.scalar_tensor_tensor(
+                out=half(res, piece), in0=src, scalar=2.0, in1=half(prod, piece), op0=ALU.mult, op1=ALU.subtract
+            )
+
+        def store(queue, piece):
+            m, v0 = (piece, 0) if piece < 2 else (piece // 2 - 1, W + W * (piece % 2))
+            queue.dma_start(out=out[m * P : (m + 1) * P, v0 : v0 + W], in_=half(res, piece))
+
+        warm = bank("warm", "second_head")
         for rep in range(WARM):
             nc.tensor.matmul_mx(
                 out=warm[0:32, :],
@@ -109,86 +145,54 @@ def tile_picked_apool_none_p_kernel(tc, x_words, x_scales, w1, w2, offs, out):
             )
 
         gather_words(early[:, 0:G], 0)
-        d_head = [bank("d_head%d" % m, "b%d" % m) for m in range(2)]
         for m in range(2):
-            mm(d_head[m][:, 0:HEAD], w1q, N + m * P, early, 0, 0, HEAD, True, False)
+            mm(half(d_head, m), w1q, m, False, 0, W, m == 0, False)
+        mm(half(base0, 0), w2q, 0, False, W, W, True, True)
+        nc.scalar.activation(out=half(held, 2), in_=half(base0, 0), func=ACT.Copy, scale=2.0)
+        for m in range(2):
+            mm(half(first_head, m), w2q, m, False, 0, W, True, True)
+        for m in range(2):
+            mm(half(d_tail[m], 0), w1q, m, False, W, W, True, False)
+        mm(half(f_tail[0], 0), w2q, 0, False, W, W, True, False)
 
         gather_words(early[:, G : 2 * G], G)
         for m in range(2):
-            mm(d_head[m][:, 0:HEAD], w1q, m * P, early, V, V, HEAD, False, True)
-        d_tail = [bank("d_tail%d" % m, "b%d" % (2 + m)) for m in range(2)]
+            mm(half(d_head, m), w1q, m, True, V, W, False, m == 1)
         for m in range(2):
-            mm(d_tail[m][:], w1q, N + m * P, early, HEAD, HEAD, G, True, False)
-
-        w2_staged = shared.tile([P, N * PACK], BF16, name="w2_staged", align_bytes=64, offset=1024)
-        cast(w2_staged[:], w2_raw[:], 0.5)
-        w2q = quantise("w2", w2_staged, N, "w2_codes")
-        w2n_staged = [keep.tile([P, P * PACK], BF16, name="w2n_staged%d" % m, align_bytes=64) for m in range(2)]
-        cast(w2n_staged[0][:], w2_raw[:, :, 0:P], -0.5)
-
-        gate_head = shared.tile([P, G], F32, name="gate_head", align_bytes=64, offset=2048)
-        gate_tail = keep.tile([P, 2 * G], F32, name="gate_tail")
-        second = keep.tile([P, 2 * V], F32, name="second")
-        first = keep.tile([P, G], F32, name="first")
-        res = keep.tile([P, 2 * V], F32, name="res")
-
-        def tanh_half(dst, src):
-            nc.scalar.activation(out=dst, in_=src, func=ACT.Tanh, scale=0.5)
-
-        def weigh(dst, c0, c1, shift, values):
-            nc.vector.scalar_tensor_tensor(
-                out=dst[:, c0:c1], in0=(gate_head[:, c0:c1] if c1 <= G else gate_tail[:, c0 - G : c1 - G]), scalar=shift, in1=values, op0=ALU.add, op1=ALU.mult
-            )
-
-        def join(engine, c0, c1):
-            engine.tensor_tensor(out=res[:, c0:c1], in0=second[:, c0:c1], in1=first[:, c0:c1], op=ALU.subtract)
-
-        head_first = bank("head_first", "b4")
-        head_second = bank("head_second", "b5")
+            tanh_half(m, half(d_head, m))
+        second_head = bank("second_head")
         for m in range(2):
-            mm(head_first[:, m * HEAD : (m + 1) * HEAD], w2q, m * P, early, 0, 0, HEAD, True, True)
+            mm(half(second_head, m), w2q, m, False, V, W, True, True)
         for m in range(2):
-            mm(head_second[:, m * HEAD : (m + 1) * HEAD], w2q, m * P, early, V, V, HEAD, True, True)
+            mm(half(d_tail[m], 1), w1q, m, False, G, W, False, False)
 
-        base = [bank("base%d" % m, "b%d" % (6 + m)) for m in range(2)]
-
-        for m in range(2):
-            tanh_half(gate_head[:, m * HEAD : (m + 1) * HEAD], d_head[m][:, 0:HEAD])
-        cast(w2n_staged[1][:], w2_raw[:, :, P : 2 * P], -0.5)
-
-        late = shared.tile([P, G], U32, name="late", align_bytes=64, offset=0)
         gather_words(late[:], 2 * G)
-        w2nq = [quantise("w2n0", w2n_staged[0], P, "word_table")]
-        weigh(first, 0, G, -1.0, head_first[:])
-        w2nq.append(quantise("w2n1", w2n_staged[1], P, "w2n1_codes"))
-        weigh(second, 0, G, 1.0, head_second[:])
+        mm(d_tail[0][:], w1q, 0, True, 2 * G, G, False, True)
+        mm(half(f_tail[0], 1), w2q, 0, False, G, W, False, False)
+        mm(f_tail[0][:], w2q, 0, True, 2 * G, G, False, True)
+        mm(d_tail[1][:], w1q, 1, True, 2 * G, G, False, True)
+        mm(half(base0, 1), w2q, 0, False, G, W, True, True)
+        mm(f_tail[1][:], w2q, 1, False, W, G, True, False)
+        mm(f_tail[1][:], w2q, 1, True, 2 * G, G, False, True)
+        base1 = bank("base1", "d_head")
+        mm(base1[:], w2q, 1, False, W, G, True, True)
+        for piece in range(2, 6):
+            tanh_half(piece, half(d_tail[piece // 2 - 1], piece % 2))
+
         for m in range(2):
-            mm(d_tail[m][:], w1q, m * P, late, 0, 2 * G, G, False, True)
-            tanh_half(gate_tail[:, m * G : (m + 1) * G], d_tail[m][:])
-        diff = [bank("diff%d" % m, "b%d" % m) for m in range(2)]
-        for m in range(2):
-            mm(diff[m][:], w2q, m * P, late, 0, 2 * G, G, True, False)
-            mm(diff[m][:], w2nq[m], 0, early, HEAD, HEAD, G, False, True)
-            mm(base[m][:], w2q, m * P, early, HEAD, HEAD, G, True, True)
-
-        def blend(c0, c1, values):
-            nc.vector.scalar_tensor_tensor(
-                out=res[:, c0:c1], in0=values, scalar=2.0, in1=second[:, c0:c1], op0=ALU.mult, op1=ALU.add
-            )
-
-        join(nc.gpsimd, 0, G)
-        nc.sync.dma_start(
-            out=out[:, 0:HEAD].rearrange("(m p) v -> p m v", p=P),
-            in_=res[:, 0:G].rearrange("p (m v) -> p m v", m=2),
-        )
-
-        weigh(second, G, 2 * G, 1.0, diff[0][:])
-        weigh(second, 2 * G, 2 * G + HEAD, 1.0, diff[1][:, 0:HEAD])
-        blend(G, 2 * G, base[0][:])
-        nc.sync.dma_start(out=out[0:P, HEAD:V], in_=res[:, G : 2 * G])
-        weigh(second, 2 * G + HEAD, 3 * G, 1.0, diff[1][:, HEAD:G])
-        for c0 in (0, HEAD):
-            blend(2 * G + c0, 2 * G + c0 + HEAD, base[1][:, c0 : c0 + HEAD])
-            nc.sync.dma_start(
-                out=out[P : 2 * P, HEAD + c0 : 2 * HEAD + c0], in_=res[:, 2 * G + c0 : 2 * G + c0 + HEAD]
-            )
+            weigh(held, m, 1.0, half(second_head, m))
+            weigh(prod, m, -1.0, half(first_head, m))
+            join_held(m)
+        store(nc.sync, 0)
+        weigh(prod, 2, 1.0, half(f_tail[0], 0))
+        join_held(2)
+        weigh(prod, 3, 1.0, half(f_tail[0], 1))
+        weigh(prod, 4, 1.0, half(f_tail[1], 0))
+        join_base(3, half(base0, 1))
+        store(nc.sync, 3)
+        weigh(prod, 5, 1.0, half(f_tail[1], 1))
+        for piece in (1, 2):
+            store(nc.scalar, piece)
+        for piece in (4, 5):
+            join_base(piece, half(base1, piece % 2))
+            store(nc.sync, piece)

@@ -28,22 +28,20 @@ def tile_picked_apool_none_p_kernel(tc, x_words, x_scales, w1, w2, offs, out):
         keep = ctx.enter_context(tc.tile_pool(name="keep", bufs=1))
         psum = ctx.enter_context(tc.psum_pool(name="psum", bufs=1))
 
-        offsets = keep.tile([P, S // 16], U16, name="offsets")
-        nc.sync.dma_start(offsets[:], offs)
-
         def load_weights(name, w):
             raw = keep.tile([P, PACK, N], F32, name=name + "_raw")
             nc.sync.dma_start(out=raw[:], in_=w.rearrange("(p j) n -> p j n", j=PACK))
             return raw
 
         w1_raw = load_weights("w1", w1)
+        offsets = keep.tile([P, S // 16], U16, name="offsets")
+        nc.sync.dma_start(offsets[:], offs)
         scale_table = keep.tile([P, T], U8, name="scale_table", align_bytes=64)
         nc.vector.memset(scale_table[:].bitcast(I32), 0)
         nc.sync.dma_start(out=scale_table[32:96:4, :].bitcast(I32), in_=x_scales[0].bitcast(I32))
-        w2_raw = load_weights("w2", w2)
-
         word_table = keep.tile([P, T], I32, name="word_table", align_bytes=64)
         nc.sync.dma_start(out=word_table[:], in_=x_words[0].rearrange("p n t -> p (n t)").bitcast(I32))
+        w2_raw = load_weights("w2", w2)
 
         picked_scales = keep.tile([P, S], U8, name="picked_scales", align_bytes=64)
         nc.gpsimd.memset(picked_scales[:].bitcast(I32), 0)
@@ -55,42 +53,54 @@ def tile_picked_apool_none_p_kernel(tc, x_words, x_scales, w1, w2, offs, out):
                 in_=spread_scales[32 + 16 * q : 48 + 16 * q : 4, :].bitcast(I32),
             )
 
-        def quantise(name, raw, factor, negate_on_vector):
-            staged = keep.tile([P, 2 * N * PACK], BF16, name=name + "_staged", align_bytes=64)
-            rows = raw[:].rearrange("p t (c i) -> p c t i", i=4)
-            plus, minus = (
-                staged[:, h * N * PACK : (h + 1) * N * PACK].rearrange("p (c i t) -> p c t i", i=4, t=PACK)
-                for h in range(2)
+        def cast(dst, src, factor):
+            nc.scalar.activation(
+                out=dst.rearrange("p (c i t) -> p c t i", i=4, t=PACK),
+                in_=src.rearrange("p t (c i) -> p c t i", i=4),
+                func=ACT.Copy,
+                scale=factor,
             )
-            nc.scalar.activation(out=plus, in_=rows, func=ACT.Copy, scale=factor)
-            if negate_on_vector:
-                nc.vector.tensor_scalar(out=minus, in0=rows, scalar1=-factor, scalar2=None, op0=ALU.mult)
-            else:
-                nc.scalar.activation(out=minus, in_=rows, func=ACT.Copy, scale=-factor)
-            codes = keep.tile([P, 2 * N], U32, name=name + "_codes", align_bytes=64)
-            scales = keep.tile([P, 2 * N], U8, name=name + "_scales", align_bytes=64)
+
+        def quantise(name, staged, width, tag):
+            codes = keep.tile([P, width], U32, name=name + "_codes", tag=tag, align_bytes=64)
+            scales = keep.tile([P, width], U8, name=name + "_scales", align_bytes=64)
             nc.vector.quantize_mx(out=codes[:].bitcast(FP8X4), scales=scales[:], in_=staged[:])
             return codes, scales
 
-        w1q = quantise("w1", w1_raw, 1.0, False)
-        w2q = quantise("w2", w2_raw, 0.5, True)
+        w1_staged = keep.tile([P, 2 * N * PACK], BF16, name="w1_staged", align_bytes=64)
+        cast(w1_staged[:, 0 : N * PACK], w1_raw[:], 1.0)
+        cast(w1_staged[:, N * PACK : 2 * N * PACK], w1_raw[:], -1.0)
+        w1q = quantise("w1", w1_staged, 2 * N, "scale_table")
+
+        w2_staged = []
+        for m in range(2):
+            staged = keep.tile([P, 2 * P * PACK], BF16, name="w2_staged%d" % m, align_bytes=64)
+            rows = w2_raw[:, :, m * P : (m + 1) * P]
+            cast(staged[:, 0 : P * PACK], rows, 0.5)
+            nc.gpsimd.tensor_scalar(
+                out=staged[:, P * PACK : 2 * P * PACK].rearrange("p (n t) -> p n t", t=PACK),
+                in0=rows.rearrange("p t n -> p n t"),
+                scalar1=-0.5,
+                scalar2=0.0,
+                op0=ALU.mult,
+                op1=ALU.add,
+            )
+            w2_staged.append(staged)
 
         early = keep.tile([P, 2 * G], U32, name="early", align_bytes=64)
-        late = keep.tile([P, G], U32, name="late", align_bytes=64)
 
         def gather_words(dst, e0):
             nc.vector.tensor_copy(
                 dst, word_table[:].bitcast(U32).indirect(offsets[:, e0 // 16 : (e0 + G) // 16])
             )
 
-        def mm(acc, weights, m, negated, e0, width, start, stop):
-            c0 = m * P + (N if negated else 0)
-            words = early[:, e0 : e0 + width] if e0 < 2 * G else late[:, e0 - 2 * G : e0 - 2 * G + width]
+        def mm(acc, weights, c0, words, e0, width, start, stop):
+            w0 = e0 % (2 * G)
             nc.tensor.matmul_mx(
                 out=acc,
                 lhsT=weights[0][:, c0 : c0 + P].bitcast(FP8X4),
                 lhsT_scale=weights[1][:, c0 : c0 + P],
-                rhs=words.bitcast(FP8X4),
+                rhs=words[:, w0 : w0 + width].bitcast(FP8X4),
                 rhs_scale=picked_scales[:, e0 : e0 + width],
                 start=start,
                 stop=stop,
@@ -102,9 +112,8 @@ def tile_picked_apool_none_p_kernel(tc, x_words, x_scales, w1, w2, offs, out):
         def half(tile, h):
             return tile[:, h * W : (h + 1) * W]
 
-        d_head, first_head = bank("d_head"), bank("first_head")
+        d_head = bank("d_head")
         d_tail = [bank("d_tail0"), bank("d_tail1")]
-        f_tail = [bank("f_tail0"), bank("f_tail1")]
         base0 = bank("base0")
 
         gate = keep.tile([P, 6 * W], F32, name="gate")
@@ -132,7 +141,7 @@ def tile_picked_apool_none_p_kernel(tc, x_words, x_scales, w1, w2, offs, out):
             m, v0 = (piece, 0) if piece < 2 else (piece // 2 - 1, W + W * (piece % 2))
             queue.dma_start(out=out[m * P : (m + 1) * P, v0 : v0 + W], in_=half(res, piece))
 
-        warm = bank("warm", "second_head")
+        warm = bank("warm", "f_tail1")
         for rep in range(WARM):
             nc.tensor.matmul_mx(
                 out=warm[0:32, :],
@@ -146,42 +155,49 @@ def tile_picked_apool_none_p_kernel(tc, x_words, x_scales, w1, w2, offs, out):
 
         gather_words(early[:, 0:G], 0)
         for m in range(2):
-            mm(half(d_head, m), w1q, m, False, 0, W, m == 0, False)
-        mm(half(base0, 0), w2q, 0, False, W, W, True, True)
-        nc.scalar.activation(out=half(held, 2), in_=half(base0, 0), func=ACT.Copy, scale=2.0)
+            mm(half(d_head, m), w1q, m * P, early, 0, W, m == 0, False)
         for m in range(2):
-            mm(half(first_head, m), w2q, m, False, 0, W, True, True)
-        for m in range(2):
-            mm(half(d_tail[m], 0), w1q, m, False, W, W, True, False)
-        mm(half(f_tail[0], 0), w2q, 0, False, W, W, True, False)
+            mm(half(d_tail[m], 0), w1q, m * P, early, W, W, True, False)
 
         gather_words(early[:, G : 2 * G], G)
         for m in range(2):
-            mm(half(d_head, m), w1q, m, True, V, W, False, m == 1)
+            mm(half(d_head, m), w1q, N + m * P, early, V, W, False, m == 1)
         for m in range(2):
             tanh_half(m, half(d_head, m))
-        second_head = bank("second_head")
         for m in range(2):
-            mm(half(second_head, m), w2q, m, False, V, W, True, True)
-        for m in range(2):
-            mm(half(d_tail[m], 1), w1q, m, False, G, W, False, False)
+            mm(half(d_tail[m], 1), w1q, m * P, early, G, W, False, False)
 
+        h_head = [bank("h_head0"), bank("h_head1")]
+        f_tail = [bank("f_tail0"), bank("f_tail1")]
+
+        def head_values(m):
+            mm(half(h_head[m], 0), w2q[m], 0, early, 0, W, True, True)
+            mm(half(h_head[m], 1), w2q[m], 0, early, V, W, True, True)
+
+        w2q = [quantise("w2_0", w2_staged[0], 2 * P, "w2_codes0")]
+        head_values(0)
+        mm(half(base0, 0), w2q[0], 0, early, W, W, True, True)
+        nc.scalar.activation(out=half(held, 2), in_=half(base0, 0), func=ACT.Copy, scale=2.0)
+        mm(f_tail[0][:], w2q[0], 0, early, W, G, True, False)
+
+        late = keep.tile([P, G], U32, name="late", tag="w2_staged0", align_bytes=64)
         gather_words(late[:], 2 * G)
-        mm(d_tail[0][:], w1q, 0, True, 2 * G, G, False, True)
-        mm(half(f_tail[0], 1), w2q, 0, False, G, W, False, False)
-        mm(f_tail[0][:], w2q, 0, True, 2 * G, G, False, True)
-        mm(d_tail[1][:], w1q, 1, True, 2 * G, G, False, True)
-        mm(half(base0, 1), w2q, 0, False, G, W, True, True)
-        mm(f_tail[1][:], w2q, 1, False, W, G, True, False)
-        mm(f_tail[1][:], w2q, 1, True, 2 * G, G, False, True)
+        w2q.append(quantise("w2_1", w2_staged[1], 2 * P, "w2_codes1"))
+        mm(d_tail[0][:], w1q, N, late, 2 * G, G, False, True)
+        head_values(1)
+        mm(f_tail[0][:], w2q[0], P, late, 2 * G, G, False, True)
+        mm(d_tail[1][:], w1q, N + P, late, 2 * G, G, False, True)
+        mm(half(base0, 1), w2q[0], 0, early, G, W, True, True)
+        mm(f_tail[1][:], w2q[1], 0, early, W, G, True, False)
+        mm(f_tail[1][:], w2q[1], P, late, 2 * G, G, False, True)
         base1 = bank("base1", "d_head")
-        mm(base1[:], w2q, 1, False, W, G, True, True)
+        mm(base1[:], w2q[1], 0, early, W, G, True, True)
         for piece in range(2, 6):
             tanh_half(piece, half(d_tail[piece // 2 - 1], piece % 2))
 
         for m in range(2):
-            weigh(held, m, 1.0, half(second_head, m))
-            weigh(prod, m, -1.0, half(first_head, m))
+            weigh(held, m, 1.0, half(h_head[m], 1))
+            weigh(prod, m, -1.0, half(h_head[m], 0))
             join_held(m)
         store(nc.sync, 0)
         weigh(prod, 2, 1.0, half(f_tail[0], 0))

@@ -19,13 +19,14 @@ P = 128
 PACK = 4
 G = 512
 W = 256
-WARM = 3
+WARM = 2
 
 
 def tile_picked_apool_none_p_kernel(tc, x_words, x_scales, w1, w2, offs, out):
     nc = tc.nc
     with ExitStack() as ctx:
         keep = ctx.enter_context(tc.tile_pool(name="keep", bufs=1))
+        shared = ctx.enter_context(tc.tile_pool(name="shared", bufs=1))
         psum = ctx.enter_context(tc.psum_pool(name="psum", bufs=1))
 
         def load_weights(name, w):
@@ -44,7 +45,7 @@ def tile_picked_apool_none_p_kernel(tc, x_words, x_scales, w1, w2, offs, out):
         w2_raw = load_weights("w2", w2)
 
         picked_scales = keep.tile([P, S], U8, name="picked_scales", align_bytes=64)
-        nc.gpsimd.memset(picked_scales[:].bitcast(I32), 0)
+        nc.vector.memset(picked_scales[:].bitcast(I32), 0)
         spread_scales = keep.tile([P, S], U8, name="spread_scales", align_bytes=64)
         nc.vector.tensor_copy(spread_scales[:], scale_table[:].indirect(offsets[:]))
         for q in (0, 2, 1, 3):
@@ -72,19 +73,26 @@ def tile_picked_apool_none_p_kernel(tc, x_words, x_scales, w1, w2, offs, out):
         cast(w1_staged[:, N * PACK : 2 * N * PACK], w1_raw[:], -1.0)
         w1q = quantise("w1", w1_staged, 2 * N, "scale_table")
 
+        minus_half = shared.tile([P, 1], F32, name="minus_half", align_bytes=64, offset=0)
+        nc.gpsimd.memset(minus_half[:], -0.5)
+        plus_half = shared.tile([P, 1], F32, name="plus_half", align_bytes=64, offset=64)
+        nc.gpsimd.memset(plus_half[:], 0.5)
         w2_staged = []
         for m in range(2):
             staged = keep.tile([P, 2 * P * PACK], BF16, name="w2_staged%d" % m, align_bytes=64)
             rows = w2_raw[:, :, m * P : (m + 1) * P]
-            cast(staged[:, 0 : P * PACK], rows, 0.5)
-            nc.gpsimd.tensor_scalar(
-                out=staged[:, P * PACK : 2 * P * PACK].rearrange("p (n t) -> p n t", t=PACK),
-                in0=rows.rearrange("p t n -> p n t"),
-                scalar1=-0.5,
-                scalar2=0.0,
-                op0=ALU.mult,
-                op1=ALU.add,
-            )
+            cast(staged[:, 0 : P * PACK], rows, plus_half[:] if m == 0 else 0.5)
+            if m == 0:
+                nc.gpsimd.tensor_scalar(
+                    out=staged[:, P * PACK : 2 * P * PACK].rearrange("p (n t) -> p n t", t=PACK),
+                    in0=rows.rearrange("p t n -> p n t"),
+                    scalar1=minus_half[:],
+                    scalar2=0.0,
+                    op0=ALU.mult,
+                    op1=ALU.add,
+                )
+            else:
+                cast(staged[:, P * PACK : 2 * P * PACK], rows, -0.5)
             w2_staged.append(staged)
 
         early = keep.tile([P, 2 * G], U32, name="early", align_bytes=64)
@@ -119,7 +127,7 @@ def tile_picked_apool_none_p_kernel(tc, x_words, x_scales, w1, w2, offs, out):
         gate = keep.tile([P, 6 * W], F32, name="gate")
         prod = keep.tile([P, 6 * W], F32, name="prod")
         res = keep.tile([P, 6 * W], F32, name="res")
-        held = keep.tile([P, 3 * W], F32, name="held")
+        held = keep.tile([P, 4 * W], F32, name="held")
 
         def tanh_half(piece, src):
             nc.scalar.activation(out=half(gate, piece), in_=src, func=ACT.Tanh, scale=-0.5)
@@ -167,47 +175,51 @@ def tile_picked_apool_none_p_kernel(tc, x_words, x_scales, w1, w2, offs, out):
         for m in range(2):
             mm(half(d_tail[m], 1), w1q, m * P, early, G, W, False, False)
 
-        h_head = [bank("h_head0"), bank("h_head1")]
-        f_tail = [bank("f_tail0"), bank("f_tail1")]
-
-        def head_values(m):
-            mm(half(h_head[m], 0), w2q[m], 0, early, 0, W, True, True)
-            mm(half(h_head[m], 1), w2q[m], 0, early, V, W, True, True)
-
         w2q = [quantise("w2_0", w2_staged[0], 2 * P, "w2_codes0")]
-        head_values(0)
-        mm(half(base0, 0), w2q[0], 0, early, W, W, True, True)
-        nc.scalar.activation(out=half(held, 2), in_=half(base0, 0), func=ACT.Copy, scale=2.0)
+        h_head0 = bank("h_head0")
+        mm(half(h_head0, 0), w2q[0], 0, early, 0, W, True, True)
+        mm(half(h_head0, 1), w2q[0], 0, early, V, W, True, True)
+        f_tail = [bank("f_tail0"), bank("f_tail1")]
         mm(f_tail[0][:], w2q[0], 0, early, W, G, True, False)
+        mm(base0[:], w2q[0], 0, early, W, G, True, True)
+        nc.scalar.activation(out=held[:, 2 * W : 4 * W], in_=base0[:], func=ACT.Copy, scale=2.0)
 
-        late = keep.tile([P, G], U32, name="late", tag="w2_staged0", align_bytes=64)
+        late = shared.tile([P, G], U32, name="late", align_bytes=64, offset=0)
         gather_words(late[:], 2 * G)
         w2q.append(quantise("w2_1", w2_staged[1], 2 * P, "w2_codes1"))
         mm(d_tail[0][:], w1q, N, late, 2 * G, G, False, True)
-        head_values(1)
+        f_head1 = bank("f_head1")
+        mm(half(f_head1, 0), w2q[1], 0, early, 0, W, True, False)
+        mm(half(f_head1, 0), w2q[1], P, early, V, W, False, True)
         mm(f_tail[0][:], w2q[0], P, late, 2 * G, G, False, True)
         mm(d_tail[1][:], w1q, N + P, late, 2 * G, G, False, True)
-        mm(half(base0, 1), w2q[0], 0, early, G, W, True, True)
-        mm(f_tail[1][:], w2q[1], 0, early, W, G, True, False)
-        mm(f_tail[1][:], w2q[1], P, late, 2 * G, G, False, True)
+        for piece in (2, 3):
+            tanh_half(piece, half(d_tail[0], piece % 2))
+        weigh(held, 0, 1.0, half(h_head0, 1))
+        weigh(prod, 0, -1.0, half(h_head0, 0))
+        join_held(0)
+        base_head1 = bank("base_head1", "h_head0")
+        mm(half(base_head1, 0), w2q[1], 0, early, 0, W, True, True)
+        f_last = [half(f_tail[1], 0), half(bank("f_end1", "d_tail0"), 0)]
+        for h in range(2):
+            mm(f_last[h], w2q[1], 0, early, W + h * W, W, True, False)
+            mm(f_last[h], w2q[1], P, late, 2 * G + h * W, W, False, True)
         base1 = bank("base1", "d_head")
         mm(base1[:], w2q[1], 0, early, W, G, True, True)
-        for piece in range(2, 6):
-            tanh_half(piece, half(d_tail[piece // 2 - 1], piece % 2))
+        for piece in (4, 5):
+            tanh_half(piece, half(d_tail[1], piece % 2))
 
-        for m in range(2):
-            weigh(held, m, 1.0, half(h_head[m], 1))
-            weigh(prod, m, -1.0, half(h_head[m], 0))
-            join_held(m)
-        store(nc.sync, 0)
+        weigh(prod, 1, 1.0, half(f_head1, 0))
         weigh(prod, 2, 1.0, half(f_tail[0], 0))
         join_held(2)
         weigh(prod, 3, 1.0, half(f_tail[0], 1))
-        weigh(prod, 4, 1.0, half(f_tail[1], 0))
-        join_base(3, half(base0, 1))
-        store(nc.sync, 3)
-        weigh(prod, 5, 1.0, half(f_tail[1], 1))
-        for piece in (1, 2):
+        join_held(3)
+        join_base(1, half(base_head1, 0))
+        for piece in (0, 1):
+            store(nc.sync, piece)
+        weigh(prod, 4, 1.0, f_last[0])
+        weigh(prod, 5, 1.0, f_last[1])
+        for piece in (2, 3):
             store(nc.scalar, piece)
         for piece in (4, 5):
             join_base(piece, half(base1, piece % 2))

@@ -62,7 +62,7 @@ def tile_picked_apool_none_p_kernel(tc, x_words, x_scales, w1, w2, offs, out):
                 scale=factor,
             )
 
-        def quantise(name, staged, width, tag):
+        def quantise(name, staged, width, tag=""):
             codes = keep.tile([P, width], U32, name=name + "_codes", tag=tag, align_bytes=64)
             scales = keep.tile([P, width], U8, name=name + "_scales", align_bytes=64)
             nc.vector.quantize_mx(out=codes[:].bitcast(FP8X4), scales=scales[:], in_=staged[:])
@@ -73,27 +73,20 @@ def tile_picked_apool_none_p_kernel(tc, x_words, x_scales, w1, w2, offs, out):
         cast(w1_staged[:, N * PACK : 2 * N * PACK], w1_raw[:], -1.0)
         w1q = quantise("w1", w1_staged, 2 * N, "scale_table")
 
-        minus_half = shared.tile([P, 1], F32, name="minus_half", align_bytes=64, offset=0)
-        nc.gpsimd.memset(minus_half[:], -0.5)
-        plus_half = shared.tile([P, 1], F32, name="plus_half", align_bytes=64, offset=64)
-        nc.gpsimd.memset(plus_half[:], 0.5)
-        w2_staged = []
-        for m in range(2):
-            staged = keep.tile([P, 2 * P * PACK], BF16, name="w2_staged%d" % m, align_bytes=64)
-            rows = w2_raw[:, :, m * P : (m + 1) * P]
-            cast(staged[:, 0 : P * PACK], rows, plus_half[:] if m == 0 else 0.5)
-            if m == 0:
-                nc.gpsimd.tensor_scalar(
-                    out=staged[:, P * PACK : 2 * P * PACK].rearrange("p (n t) -> p n t", t=PACK),
-                    in0=rows.rearrange("p t n -> p n t"),
-                    scalar1=minus_half[:],
-                    scalar2=0.0,
-                    op0=ALU.mult,
-                    op1=ALU.add,
-                )
-            else:
-                cast(staged[:, P * PACK : 2 * P * PACK], rows, -0.5)
-            w2_staged.append(staged)
+        one_half = shared.tile([P, 1], F32, name="one_half", align_bytes=64, offset=0)
+        nc.gpsimd.memset(one_half[:], 0.5)
+        plus_staged = keep.tile([P, N * PACK], BF16, name="plus_staged", align_bytes=64)
+        cast(plus_staged[:, 0 : P * PACK], w2_raw[:, :, 0:P], one_half[:])
+        nc.gpsimd.tensor_scalar(
+            out=plus_staged[:, P * PACK : N * PACK].rearrange("p (n t) -> p n t", t=PACK),
+            in0=w2_raw[:, :, P:N].rearrange("p t n -> p n t"),
+            scalar1=one_half[:],
+            scalar2=0.0,
+            op0=ALU.mult,
+            op1=ALU.add,
+        )
+        minus_staged = keep.tile([P, N * PACK], BF16, name="minus_staged", align_bytes=64)
+        cast(minus_staged[:], w2_raw[:], -0.5)
 
         early = keep.tile([P, 2 * G], U32, name="early", align_bytes=64)
 
@@ -131,6 +124,9 @@ def tile_picked_apool_none_p_kernel(tc, x_words, x_scales, w1, w2, offs, out):
 
         def tanh_half(piece, src):
             nc.scalar.activation(out=half(gate, piece), in_=src, func=ACT.Tanh, scale=-0.5)
+
+        def hold(piece, src):
+            nc.scalar.activation(out=half(held, piece), in_=src, func=ACT.Copy, scale=2.0)
 
         def weigh(dst, piece, shift, src):
             nc.vector.scalar_tensor_tensor(
@@ -172,53 +168,52 @@ def tile_picked_apool_none_p_kernel(tc, x_words, x_scales, w1, w2, offs, out):
             mm(half(d_head, m), w1q, N + m * P, early, V, W, False, m == 1)
         for m in range(2):
             tanh_half(m, half(d_head, m))
-        for m in range(2):
-            mm(half(d_tail[m], 1), w1q, m * P, early, G, W, False, False)
+        mm(half(d_tail[0], 1), w1q, 0, early, G, W, False, False)
 
-        w2q = [quantise("w2_0", w2_staged[0], 2 * P, "w2_codes0")]
+        plus = quantise("plus", plus_staged, N)
         h_head0 = bank("h_head0")
-        mm(half(h_head0, 0), w2q[0], 0, early, 0, W, True, True)
-        mm(half(h_head0, 1), w2q[0], 0, early, V, W, True, True)
+        mm(half(h_head0, 0), plus, 0, early, 0, W, True, True)
+        mm(half(h_head0, 1), plus, 0, early, V, W, True, True)
+        f_head1 = bank("f_head1")
+        mm(half(f_head1, 0), plus, P, early, 0, W, True, False)
+        mm(half(f_head1, 1), plus, P, early, 0, W, False, False)
+        mm(half(base0, 0), plus, 0, early, W, W, True, True)
+        hold(2, half(base0, 0))
         f_tail = [bank("f_tail0"), bank("f_tail1")]
-        mm(f_tail[0][:], w2q[0], 0, early, W, G, True, False)
-        mm(base0[:], w2q[0], 0, early, W, G, True, True)
-        nc.scalar.activation(out=held[:, 2 * W : 4 * W], in_=base0[:], func=ACT.Copy, scale=2.0)
+        mm(f_tail[0][:], plus, 0, early, W, G, True, False)
 
         late = shared.tile([P, G], U32, name="late", align_bytes=64, offset=0)
         gather_words(late[:], 2 * G)
-        w2q.append(quantise("w2_1", w2_staged[1], 2 * P, "w2_codes1"))
+        minus = quantise("minus", minus_staged, N)
         mm(d_tail[0][:], w1q, N, late, 2 * G, G, False, True)
-        f_head1 = bank("f_head1")
-        mm(half(f_head1, 0), w2q[1], 0, early, 0, W, True, False)
-        mm(half(f_head1, 0), w2q[1], P, early, V, W, False, True)
-        mm(f_tail[0][:], w2q[0], P, late, 2 * G, G, False, True)
+        mm(half(f_head1, 0), minus, P, early, V, W, False, True)
+        mm(f_tail[0][:], minus, 0, late, 2 * G, G, False, True)
+        mm(half(base0, 1), plus, 0, early, G, W, True, True)
+        mm(half(d_tail[1], 1), w1q, P, early, G, W, False, False)
         mm(d_tail[1][:], w1q, N + P, late, 2 * G, G, False, True)
+        mm(f_tail[1][:], plus, P, early, W, G, True, False)
+        mm(f_tail[1][:], minus, P, late, 2 * G, G, False, True)
+        base1 = bank("base1", "d_head")
+        mm(base1[:], plus, P, early, W, G, True, True)
         for piece in (2, 3):
             tanh_half(piece, half(d_tail[0], piece % 2))
-        weigh(held, 0, 1.0, half(h_head0, 1))
-        weigh(prod, 0, -1.0, half(h_head0, 0))
-        join_held(0)
-        base_head1 = bank("base_head1", "h_head0")
-        mm(half(base_head1, 0), w2q[1], 0, early, 0, W, True, True)
-        f_last = [half(f_tail[1], 0), half(bank("f_end1", "d_tail0"), 0)]
-        for h in range(2):
-            mm(f_last[h], w2q[1], 0, early, W + h * W, W, True, False)
-            mm(f_last[h], w2q[1], P, late, 2 * G + h * W, W, False, True)
-        base1 = bank("base1", "d_head")
-        mm(base1[:], w2q[1], 0, early, W, G, True, True)
+        hold(3, half(base0, 1))
         for piece in (4, 5):
             tanh_half(piece, half(d_tail[1], piece % 2))
 
+        weigh(held, 0, 1.0, half(h_head0, 1))
+        weigh(prod, 0, -1.0, half(h_head0, 0))
+        join_held(0)
         weigh(prod, 1, 1.0, half(f_head1, 0))
         weigh(prod, 2, 1.0, half(f_tail[0], 0))
         join_held(2)
         weigh(prod, 3, 1.0, half(f_tail[0], 1))
         join_held(3)
-        join_base(1, half(base_head1, 0))
+        join_base(1, half(f_head1, 1))
         for piece in (0, 1):
             store(nc.sync, piece)
-        weigh(prod, 4, 1.0, f_last[0])
-        weigh(prod, 5, 1.0, f_last[1])
+        weigh(prod, 4, 1.0, half(f_tail[1], 0))
+        weigh(prod, 5, 1.0, half(f_tail[1], 1))
         for piece in (2, 3):
             store(nc.scalar, piece)
         for piece in (4, 5):

@@ -62,8 +62,8 @@ def tile_picked_apool_none_p_kernel(tc, x_words, x_scales, w1, w2, offs, out):
                 scale=factor,
             )
 
-        def quantise(name, staged, width, tag=""):
-            codes = keep.tile([P, width], U32, name=name + "_codes", tag=tag, align_bytes=64)
+        def quantise(name, staged, width):
+            codes = keep.tile([P, width], U32, name=name + "_codes", align_bytes=64)
             scales = keep.tile([P, width], U8, name=name + "_scales", align_bytes=64)
             nc.vector.quantize_mx(out=codes[:].bitcast(FP8X4), scales=scales[:], in_=staged[:])
             return codes, scales
@@ -71,7 +71,7 @@ def tile_picked_apool_none_p_kernel(tc, x_words, x_scales, w1, w2, offs, out):
         w1_staged = keep.tile([P, 2 * N * PACK], BF16, name="w1_staged", align_bytes=64)
         cast(w1_staged[:, 0 : N * PACK], w1_raw[:], 1.0)
         cast(w1_staged[:, N * PACK : 2 * N * PACK], w1_raw[:], -1.0)
-        w1q = quantise("w1", w1_staged, 2 * N, "scale_table")
+        w1q = quantise("w1", w1_staged, 2 * N)
 
         one_half = shared.tile([P, 1], F32, name="one_half", align_bytes=64, offset=0)
         nc.gpsimd.memset(one_half[:], 0.5)

@@ -20,6 +20,7 @@ PACK = 4
 G = 512
 W = 256
 WARM = 2
+SPLIT = 160
 
 
 def tile_picked_apool_none_p_kernel(tc, x_words, x_scales, w1, w2, offs, out):
@@ -76,10 +77,10 @@ def tile_picked_apool_none_p_kernel(tc, x_words, x_scales, w1, w2, offs, out):
         one_half = shared.tile([P, 1], F32, name="one_half", align_bytes=64, offset=0)
         nc.gpsimd.memset(one_half[:], 0.5)
         plus_staged = keep.tile([P, N * PACK], BF16, name="plus_staged", align_bytes=64)
-        cast(plus_staged[:, 0 : P * PACK], w2_raw[:, :, 0:P], one_half[:])
+        cast(plus_staged[:, 0 : SPLIT * PACK], w2_raw[:, :, 0:SPLIT], one_half[:])
         nc.gpsimd.tensor_scalar(
-            out=plus_staged[:, P * PACK : N * PACK].rearrange("p (n t) -> p n t", t=PACK),
-            in0=w2_raw[:, :, P:N].rearrange("p t n -> p n t"),
+            out=plus_staged[:, SPLIT * PACK : N * PACK].rearrange("p (n t) -> p n t", t=PACK),
+            in0=w2_raw[:, :, SPLIT:N].rearrange("p t n -> p n t"),
             scalar1=one_half[:],
             scalar2=0.0,
             op0=ALU.mult,
@@ -115,12 +116,12 @@ def tile_picked_apool_none_p_kernel(tc, x_words, x_scales, w1, w2, offs, out):
 
         d_head = bank("d_head")
         d_tail = [bank("d_tail0"), bank("d_tail1")]
-        base0 = bank("base0")
+        base_held = bank("base_held")
 
         gate = keep.tile([P, 6 * W], F32, name="gate")
         prod = keep.tile([P, 6 * W], F32, name="prod")
         res = keep.tile([P, 6 * W], F32, name="res")
-        held = keep.tile([P, 4 * W], F32, name="held")
+        held = keep.tile([P, 6 * W], F32, name="held")
 
         def tanh_half(piece, src):
             nc.scalar.activation(out=half(gate, piece), in_=src, func=ACT.Tanh, scale=-0.5)
@@ -128,22 +129,34 @@ def tile_picked_apool_none_p_kernel(tc, x_words, x_scales, w1, w2, offs, out):
         def hold(piece, src):
             nc.scalar.activation(out=half(held, piece), in_=src, func=ACT.Copy, scale=2.0)
 
-        def weigh(dst, piece, shift, src):
+        def weigh(dst, piece, shift, src, cols=slice(0, W)):
             nc.vector.scalar_tensor_tensor(
-                out=half(dst, piece), in0=half(gate, piece), scalar=shift, in1=src, op0=ALU.add, op1=ALU.mult
+                out=half(dst, piece)[:, cols],
+                in0=half(gate, piece)[:, cols],
+                scalar=shift,
+                in1=src[:, cols],
+                op0=ALU.add,
+                op1=ALU.mult,
             )
 
         def join_held(piece):
             nc.gpsimd.tensor_tensor(out=half(res, piece), in0=half(held, piece), in1=half(prod, piece), op=ALU.subtract)
 
-        def join_base(piece, src):
+        def join_base(piece, src, cols=slice(0, W)):
             nc.vector.scalar_tensor_tensor(
-                out=half(res, piece), in0=src, scalar=2.0, in1=half(prod, piece), op0=ALU.mult, op1=ALU.subtract
+                out=half(res, piece)[:, cols],
+                in0=src[:, cols],
+                scalar=2.0,
+                in1=half(prod, piece)[:, cols],
+                op0=ALU.mult,
+                op1=ALU.subtract,
             )
 
-        def store(queue, piece):
+        def store(queue, piece, cols=slice(0, W)):
             m, v0 = (piece, 0) if piece < 2 else (piece // 2 - 1, W + W * (piece % 2))
-            queue.dma_start(out=out[m * P : (m + 1) * P, v0 : v0 + W], in_=half(res, piece))
+            queue.dma_start(
+                out=out[m * P : (m + 1) * P, v0 + cols.start : v0 + cols.stop], in_=half(res, piece)[:, cols]
+            )
 
         warm = bank("warm", "f_tail1")
         for rep in range(WARM):
@@ -168,7 +181,8 @@ def tile_picked_apool_none_p_kernel(tc, x_words, x_scales, w1, w2, offs, out):
             mm(half(d_head, m), w1q, N + m * P, early, V, W, False, m == 1)
         for m in range(2):
             tanh_half(m, half(d_head, m))
-        mm(half(d_tail[0], 1), w1q, 0, early, G, W, False, False)
+        for m in range(2):
+            mm(half(d_tail[m], 1), w1q, m * P, early, G, W, False, False)
 
         plus = quantise("plus", plus_staged, N)
         h_head0 = bank("h_head0")
@@ -177,8 +191,6 @@ def tile_picked_apool_none_p_kernel(tc, x_words, x_scales, w1, w2, offs, out):
         f_head1 = bank("f_head1")
         mm(half(f_head1, 0), plus, P, early, 0, W, True, False)
         mm(half(f_head1, 1), plus, P, early, 0, W, False, False)
-        mm(half(base0, 0), plus, 0, early, W, W, True, True)
-        hold(2, half(base0, 0))
         f_tail = [bank("f_tail0"), bank("f_tail1")]
         mm(f_tail[0][:], plus, 0, early, W, G, True, False)
 
@@ -188,18 +200,20 @@ def tile_picked_apool_none_p_kernel(tc, x_words, x_scales, w1, w2, offs, out):
         mm(d_tail[0][:], w1q, N, late, 2 * G, G, False, True)
         mm(half(f_head1, 0), minus, P, early, V, W, False, True)
         mm(f_tail[0][:], minus, 0, late, 2 * G, G, False, True)
-        mm(half(base0, 1), plus, 0, early, G, W, True, True)
-        mm(half(d_tail[1], 1), w1q, P, early, G, W, False, False)
+        mm(half(base_held, 0), plus, 0, early, W, W, True, True)
         mm(d_tail[1][:], w1q, N + P, late, 2 * G, G, False, True)
         mm(f_tail[1][:], plus, P, early, W, G, True, False)
         mm(f_tail[1][:], minus, P, late, 2 * G, G, False, True)
-        base1 = bank("base1", "d_head")
-        mm(base1[:], plus, P, early, W, G, True, True)
         for piece in (2, 3):
             tanh_half(piece, half(d_tail[0], piece % 2))
-        hold(3, half(base0, 1))
+        hold(2, half(base_held, 0))
+        mm(half(base_held, 1), plus, P, early, W, W, True, True)
+        base_end = bank("base_end", "d_head")
+        for m in range(2):
+            mm(half(base_end, m), plus, m * P, early, G, W, True, True)
         for piece in (4, 5):
             tanh_half(piece, half(d_tail[1], piece % 2))
+        hold(4, half(base_held, 1))
 
         weigh(held, 0, 1.0, half(h_head0, 1))
         weigh(prod, 0, -1.0, half(h_head0, 0))
@@ -207,15 +221,19 @@ def tile_picked_apool_none_p_kernel(tc, x_words, x_scales, w1, w2, offs, out):
         weigh(prod, 1, 1.0, half(f_head1, 0))
         weigh(prod, 2, 1.0, half(f_tail[0], 0))
         join_held(2)
-        weigh(prod, 3, 1.0, half(f_tail[0], 1))
-        join_held(3)
         join_base(1, half(f_head1, 1))
         for piece in (0, 1):
             store(nc.sync, piece)
+        weigh(prod, 3, 1.0, half(f_tail[0], 1))
         weigh(prod, 4, 1.0, half(f_tail[1], 0))
-        weigh(prod, 5, 1.0, half(f_tail[1], 1))
+        join_held(4)
+        join_base(3, half(base_end, 0))
         for piece in (2, 3):
-            store(nc.scalar, piece)
-        for piece in (4, 5):
-            join_base(piece, half(base1, piece % 2))
             store(nc.sync, piece)
+        store(nc.scalar, 4)
+        last_parts = (slice(0, W // 2), slice(W // 2, W))
+        for cols in last_parts:
+            weigh(prod, 5, 1.0, half(f_tail[1], 1), cols)
+        for cols in last_parts:
+            join_base(5, half(base_end, 1), cols)
+            store(nc.sync, 5, cols)

@@ -152,11 +152,9 @@ def tile_picked_apool_none_p_kernel(tc, x_words, x_scales, w1, w2, offs, out):
                 op1=ALU.subtract,
             )
 
-        def store(queue, piece, cols=slice(0, W)):
-            m, v0 = (piece, 0) if piece < 2 else (piece // 2 - 1, W + W * (piece % 2))
-            queue.dma_start(
-                out=out[m * P : (m + 1) * P, v0 + cols.start : v0 + cols.stop], in_=half(res, piece)[:, cols]
-            )
+        def store_tail(m, v0, v1):
+            c0 = 2 * W + m * G - W
+            nc.sync.dma_start(out=out[m * P : (m + 1) * P, v0:v1], in_=res[:, c0 + v0 : c0 + v1])
 
         warm = bank("warm", "f_tail1")
         for rep in range(WARM):
@@ -222,18 +220,19 @@ def tile_picked_apool_none_p_kernel(tc, x_words, x_scales, w1, w2, offs, out):
         weigh(prod, 2, 1.0, half(f_tail[0], 0))
         join_held(2)
         join_base(1, half(f_head1, 1))
-        for piece in (0, 1):
-            store(nc.sync, piece)
+        nc.sync.dma_start(
+            out=out[:, 0:W].rearrange("(m p) v -> p m v", p=P),
+            in_=res[:, 0 : 2 * W].rearrange("p (m v) -> p m v", m=2),
+        )
         weigh(prod, 3, 1.0, half(f_tail[0], 1))
         weigh(prod, 4, 1.0, half(f_tail[1], 0))
         join_held(4)
         join_base(3, half(base_end, 0))
-        for piece in (2, 3):
-            store(nc.sync, piece)
-        store(nc.scalar, 4)
+        store_tail(0, W, G)
+        store_tail(0, G, V)
         last_parts = (slice(0, W // 2), slice(W // 2, W))
         for cols in last_parts:
             weigh(prod, 5, 1.0, half(f_tail[1], 1), cols)
         for cols in last_parts:
             join_base(5, half(base_end, 1), cols)
-            store(nc.sync, 5, cols)
+        store_tail(1, W, V)

@@ -86,8 +86,8 @@ def tile_picked_apool_none_p_kernel(tc, x_words, x_scales, w1, w2, offs, out):
             op0=ALU.mult,
             op1=ALU.add,
         )
-        minus_staged = keep.tile([P, N * PACK], BF16, name="minus_staged", align_bytes=64)
-        cast(minus_staged[:], w2_raw[:], -0.5)
+        minus_staged = [keep.tile([P, P * PACK], BF16, name="minus_staged%d" % m, align_bytes=64) for m in range(2)]
+        cast(minus_staged[0][:], w2_raw[:, :, 0:P], -0.5)
 
         early = keep.tile([P, 2 * G], U32, name="early", align_bytes=64)
 
@@ -177,31 +177,36 @@ def tile_picked_apool_none_p_kernel(tc, x_words, x_scales, w1, w2, offs, out):
         gather_words(early[:, G : 2 * G], G)
         for m in range(2):
             mm(half(d_head, m), w1q, N + m * P, early, V, W, False, m == 1)
-        for m in range(2):
-            tanh_half(m, half(d_head, m))
+        tanh_half(1, half(d_head, 1))
+        cast(minus_staged[1][:], w2_raw[:, :, P:N], -0.5)
+        tanh_half(0, half(d_head, 0))
         for m in range(2):
             mm(half(d_tail[m], 1), w1q, m * P, early, G, W, False, False)
 
         plus = quantise("plus", plus_staged, N)
         h_head0 = bank("h_head0")
-        mm(half(h_head0, 0), plus, 0, early, 0, W, True, True)
-        mm(half(h_head0, 1), plus, 0, early, V, W, True, True)
+        mm(half(h_head0, 0), plus, P, early, 0, W, True, True)
+        mm(half(h_head0, 1), plus, P, early, V, W, True, True)
         f_head1 = bank("f_head1")
-        mm(half(f_head1, 0), plus, P, early, 0, W, True, False)
-        mm(half(f_head1, 1), plus, P, early, 0, W, False, False)
+        mm(half(f_head1, 0), plus, 0, early, 0, W, True, False)
+        mm(half(f_head1, 1), plus, 0, early, 0, W, False, False)
         f_tail = [bank("f_tail0"), bank("f_tail1")]
         mm(f_tail[0][:], plus, 0, early, W, G, True, False)
 
         late = shared.tile([P, G], U32, name="late", align_bytes=64, offset=0)
         gather_words(late[:], 2 * G)
-        minus = quantise("minus", minus_staged, N)
+        minus = [quantise("minus0", minus_staged[0], P)]
+        weigh(held, 1, 1.0, half(h_head0, 1))
+        weigh(prod, 1, -1.0, half(h_head0, 0))
+        join_held(1)
+        minus.append(quantise("minus1", minus_staged[1], P))
         mm(d_tail[0][:], w1q, N, late, 2 * G, G, False, True)
-        mm(half(f_head1, 0), minus, P, early, V, W, False, True)
-        mm(f_tail[0][:], minus, 0, late, 2 * G, G, False, True)
+        mm(half(f_head1, 0), minus[0], 0, early, V, W, False, True)
+        mm(f_tail[0][:], minus[0], 0, late, 2 * G, G, False, True)
         mm(half(base_held, 0), plus, 0, early, W, W, True, True)
         mm(d_tail[1][:], w1q, N + P, late, 2 * G, G, False, True)
         mm(f_tail[1][:], plus, P, early, W, G, True, False)
-        mm(f_tail[1][:], minus, P, late, 2 * G, G, False, True)
+        mm(f_tail[1][:], minus[1], 0, late, 2 * G, G, False, True)
         for piece in (2, 3):
             tanh_half(piece, half(d_tail[0], piece % 2))
         hold(2, half(base_held, 0))
@@ -213,13 +218,10 @@ def tile_picked_apool_none_p_kernel(tc, x_words, x_scales, w1, w2, offs, out):
             tanh_half(piece, half(d_tail[1], piece % 2))
         hold(4, half(base_held, 1))
 
-        weigh(held, 0, 1.0, half(h_head0, 1))
-        weigh(prod, 0, -1.0, half(h_head0, 0))
-        join_held(0)
-        weigh(prod, 1, 1.0, half(f_head1, 0))
+        weigh(prod, 0, 1.0, half(f_head1, 0))
         weigh(prod, 2, 1.0, half(f_tail[0], 0))
         join_held(2)
-        join_base(1, half(f_head1, 1))
+        join_base(0, half(f_head1, 1))
         nc.sync.dma_start(
             out=out[:, 0:W].rearrange("(m p) v -> p m v", p=P),
             in_=res[:, 0 : 2 * W].rearrange("p (m v) -> p m v", m=2),

@@ -152,9 +152,9 @@ def tile_picked_apool_none_p_kernel(tc, x_words, x_scales, w1, w2, offs, out):
                 op1=ALU.subtract,
             )
 
-        def store_tail(m, v0, v1):
+        def store_tail(queue, m, v0, v1):
             c0 = 2 * W + m * G - W
-            nc.sync.dma_start(out=out[m * P : (m + 1) * P, v0:v1], in_=res[:, c0 + v0 : c0 + v1])
+            queue.dma_start(out=out[m * P : (m + 1) * P, v0:v1], in_=res[:, c0 + v0 : c0 + v1])
 
         warm = bank("warm", "f_tail1")
         for rep in range(WARM):
@@ -216,7 +216,7 @@ def tile_picked_apool_none_p_kernel(tc, x_words, x_scales, w1, w2, offs, out):
             mm(half(base_end, m), plus, m * P, early, G, W, True, True)
         for piece in (4, 5):
             tanh_half(piece, half(d_tail[1], piece % 2))
-        hold(4, half(base_held, 1))
+        nc.scalar.activation(out=half(held, 4)[:, 0:P], in_=half(base_held, 1)[:, 0:P], func=ACT.Copy, scale=2.0)
 
         weigh(prod, 0, 1.0, half(f_head1, 0))
         weigh(prod, 2, 1.0, half(f_tail[0], 0))
@@ -228,13 +228,14 @@ def tile_picked_apool_none_p_kernel(tc, x_words, x_scales, w1, w2, offs, out):
         )
         weigh(prod, 3, 1.0, half(f_tail[0], 1))
         weigh(prod, 4, 1.0, half(f_tail[1], 0))
-        join_held(4)
+        nc.gpsimd.tensor_tensor(
+            out=half(res, 4)[:, 0:P], in0=half(held, 4)[:, 0:P], in1=half(prod, 4)[:, 0:P], op=ALU.subtract
+        )
         join_base(3, half(base_end, 0))
-        store_tail(0, W, G)
-        store_tail(0, G, V)
-        last_parts = (slice(0, W // 2), slice(W // 2, W))
-        for cols in last_parts:
-            weigh(prod, 5, 1.0, half(f_tail[1], 1), cols)
-        for cols in last_parts:
-            join_base(5, half(base_end, 1), cols)
-        store_tail(1, W, V)
+        store_tail(nc.sync, 0, W, G)
+        store_tail(nc.sync, 0, G, V)
+        weigh(prod, 5, 1.0, half(f_tail[1], 1))
+        join_base(4, half(base_held, 1), slice(P, W))
+        store_tail(nc.sync, 1, W, G)
+        join_base(5, half(base_end, 1))
+        store_tail(nc.scalar, 1, G, V)

@@ -38,16 +38,16 @@ def tile_picked_apool_none_p_kernel(tc, x_words, x_scales, w1, w2, offs, out):
         w1_raw = load_weights("w1", w1)
         offsets = keep.tile([P, S // 16], U16, name="offsets")
         nc.sync.dma_start(offsets[:], offs)
-        scale_table = keep.tile([P, T], U8, name="scale_table", align_bytes=64)
+        scale_table = keep.tile([P, T], U8, name="scale_table", align_bytes=256)
         nc.vector.memset(scale_table[:].bitcast(I32), 0)
         nc.sync.dma_start(out=scale_table[32:96:4, :].bitcast(I32), in_=x_scales[0].bitcast(I32))
-        word_table = keep.tile([P, T], I32, name="word_table", align_bytes=64)
+        word_table = keep.tile([P, T], I32, name="word_table", align_bytes=256)
         nc.sync.dma_start(out=word_table[:], in_=x_words[0].rearrange("p n t -> p (n t)").bitcast(I32))
         w2_raw = load_weights("w2", w2)
 
-        picked_scales = keep.tile([P, S], U8, name="picked_scales", align_bytes=64)
+        picked_scales = keep.tile([P, S], U8, name="picked_scales", align_bytes=256)
         nc.vector.memset(picked_scales[:].bitcast(I32), 0)
-        spread_scales = keep.tile([P, S], U8, name="spread_scales", align_bytes=64)
+        spread_scales = keep.tile([P, S], U8, name="spread_scales", align_bytes=256)
         nc.vector.tensor_copy(spread_scales[:], scale_table[:].indirect(offsets[:]))
         for q in (0, 2, 1, 3):
             nc.sync.dma_start(
@@ -64,19 +64,19 @@ def tile_picked_apool_none_p_kernel(tc, x_words, x_scales, w1, w2, offs, out):
             )
 
         def quantise(name, staged, width):
-            codes = keep.tile([P, width], U32, name=name + "_codes", align_bytes=64)
-            scales = keep.tile([P, width], U8, name=name + "_scales", align_bytes=64)
+            codes = keep.tile([P, width], U32, name=name + "_codes", align_bytes=256)
+            scales = keep.tile([P, width], U8, name=name + "_scales", align_bytes=256)
             nc.vector.quantize_mx(out=codes[:].bitcast(FP8X4), scales=scales[:], in_=staged[:])
             return codes, scales
 
-        w1_staged = keep.tile([P, 2 * N * PACK], BF16, name="w1_staged", align_bytes=64)
+        w1_staged = keep.tile([P, 2 * N * PACK], BF16, name="w1_staged", align_bytes=256)
         cast(w1_staged[:, 0 : N * PACK], w1_raw[:], 1.0)
         cast(w1_staged[:, N * PACK : 2 * N * PACK], w1_raw[:], -1.0)
         w1q = quantise("w1", w1_staged, 2 * N)
 
-        one_half = shared.tile([P, 1], F32, name="one_half", align_bytes=64, offset=0)
+        one_half = shared.tile([P, 1], F32, name="one_half", align_bytes=256, offset=0)
         nc.gpsimd.memset(one_half[:], 0.5)
-        plus_staged = keep.tile([P, N * PACK], BF16, name="plus_staged", align_bytes=64)
+        plus_staged = keep.tile([P, N * PACK], BF16, name="plus_staged", align_bytes=256)
         cast(plus_staged[:, 0 : SPLIT * PACK], w2_raw[:, :, 0:SPLIT], one_half[:])
         nc.gpsimd.tensor_scalar(
             out=plus_staged[:, SPLIT * PACK : N * PACK].rearrange("p (n t) -> p n t", t=PACK),
@@ -86,10 +86,10 @@ def tile_picked_apool_none_p_kernel(tc, x_words, x_scales, w1, w2, offs, out):
             op0=ALU.mult,
             op1=ALU.add,
         )
-        minus_staged = [keep.tile([P, P * PACK], BF16, name="minus_staged%d" % m, align_bytes=64) for m in range(2)]
+        minus_staged = [keep.tile([P, P * PACK], BF16, name="minus_staged%d" % m, align_bytes=256) for m in range(2)]
         cast(minus_staged[0][:], w2_raw[:, :, 0:P], -0.5)
 
-        early = keep.tile([P, 2 * G], U32, name="early", align_bytes=64)
+        early = keep.tile([P, 2 * G], U32, name="early", align_bytes=256)
 
         def gather_words(dst, e0):
             nc.vector.tensor_copy(
@@ -193,7 +193,7 @@ def tile_picked_apool_none_p_kernel(tc, x_words, x_scales, w1, w2, offs, out):
         f_tail = [bank("f_tail0"), bank("f_tail1")]
         mm(f_tail[0][:], plus, 0, early, W, G, True, False)
 
-        late = shared.tile([P, G], U32, name="late", align_bytes=64, offset=0)
+        late = shared.tile([P, G], U32, name="late", align_bytes=256, offset=0)
         gather_words(late[:], 2 * G)
         minus = [quantise("minus0", minus_staged[0], P)]
         weigh(held, 1, 1.0, half(h_head0, 1))

from contextlib import ExitStack

import concourse.mybir as mybir

K, T, S, V, N = 512, 4096, 1536, 768, 256
FLOPS = 2 * 2 * K * N * S

F32 = mybir.dt.float32
BF16 = mybir.dt.bfloat16
I32 = mybir.dt.int32
U32 = mybir.dt.uint32
U16 = mybir.dt.uint16
U8 = mybir.dt.uint8
FP8X4 = mybir.dt.float8_e4m3fn_x4
ACT = mybir.ActivationFunctionType
ALU = mybir.AluOpType

P = 128
PACK = 4
G = 512
W = 256
WARM = 2
SPLIT = 160


def tile_picked_apool_none_p_kernel(tc, x_words, x_scales, w1, w2, offs, out):
    nc = tc.nc
    with ExitStack() as ctx:
        keep = ctx.enter_context(tc.tile_pool(name="keep", bufs=1))
        shared = ctx.enter_context(tc.tile_pool(name="shared", bufs=1))
        psum = ctx.enter_context(tc.psum_pool(name="psum", bufs=1))

        def load_weights(name, w):
            raw = keep.tile([P, PACK, N], F32, name=name + "_raw")
            nc.sync.dma_start(out=raw[:], in_=w.rearrange("(p j) n -> p j n", j=PACK))
            return raw

        w1_raw = load_weights("w1", w1)
        offsets = keep.tile([P, S // 16], U16, name="offsets")
        nc.sync.dma_start(offsets[:], offs)
        scale_table = keep.tile([P, T], U8, name="scale_table", align_bytes=256)
        nc.vector.memset(scale_table[:].bitcast(I32), 0)
        nc.sync.dma_start(out=scale_table[32:96:4, :].bitcast(I32), in_=x_scales[0].bitcast(I32))
        word_table = keep.tile([P, T], I32, name="word_table", align_bytes=256)
        nc.sync.dma_start(out=word_table[:], in_=x_words[0].rearrange("p n t -> p (n t)").bitcast(I32))
        w2_raw = load_weights("w2", w2)

        picked_scales = keep.tile([P, S], U8, name="picked_scales", align_bytes=256)
        nc.vector.memset(picked_scales[:].bitcast(I32), 0)
        spread_scales = keep.tile([P, S], U8, name="spread_scales", align_bytes=256)
        nc.vector.tensor_copy(spread_scales[:], scale_table[:].indirect(offsets[:]))
        for q in (0, 2, 1, 3):
            nc.sync.dma_start(
                out=picked_scales[32 * q : 32 * q + 4, :].bitcast(I32),
                in_=spread_scales[32 + 16 * q : 48 + 16 * q : 4, :].bitcast(I32),
            )

        def cast(dst, src, factor):
            nc.scalar.activation(
                out=dst.rearrange("p (c i t) -> p c t i", i=4, t=PACK),
                in_=src.rearrange("p t (c i) -> p c t i", i=4),
                func=ACT.Copy,
                scale=factor,
            )

        def quantise(name, staged, width):
            codes = keep.tile([P, width], U32, name=name + "_codes", align_bytes=256)
            scales = keep.tile([P, width], U8, name=name + "_scales", align_bytes=256)
            nc.vector.quantize_mx(out=codes[:].bitcast(FP8X4), scales=scales[:], in_=staged[:])
            return codes, scales

        w1_staged = keep.tile([P, 2 * N * PACK], BF16, name="w1_staged", align_bytes=256)
        cast(w1_staged[:, 0 : N * PACK], w1_raw[:], 1.0)
        cast(w1_staged[:, N * PACK : 2 * N * PACK], w1_raw[:], -1.0)
        w1q = quantise("w1", w1_staged, 2 * N)

        one_half = shared.tile([P, 1], F32, name="one_half", align_bytes=256, offset=0)
        nc.gpsimd.memset(one_half[:], 0.5)
        plus_staged = keep.tile([P, N * PACK], BF16, name="plus_staged", align_bytes=256)
        cast(plus_staged[:, 0 : SPLIT * PACK], w2_raw[:, :, 0:SPLIT], one_half[:])
        nc.gpsimd.tensor_scalar(
            out=plus_staged[:, SPLIT * PACK : N * PACK].rearrange("p (n t) -> p n t", t=PACK),
            in0=w2_raw[:, :, SPLIT:N].rearrange("p t n -> p n t"),
            scalar1=one_half[:],
            scalar2=0.0,
            op0=ALU.mult,
            op1=ALU.add,
        )
        minus_staged = [keep.tile([P, P * PACK], BF16, name="minus_staged%d" % m, align_bytes=256) for m in range(2)]
        cast(minus_staged[0][:], w2_raw[:, :, 0:P], -0.5)

        early = keep.tile([P, 2 * G], U32, name="early", align_bytes=256)

        def gather_words(dst, e0):
            nc.vector.tensor_copy(
                dst, word_table[:].bitcast(U32).indirect(offsets[:, e0 // 16 : (e0 + G) // 16])
            )

        def mm(acc, weights, c0, words, e0, width, start, stop):
            w0 = e0 % (2 * G)
            nc.tensor.matmul_mx(
                out=acc,
                lhsT=weights[0][:, c0 : c0 + P].bitcast(FP8X4),
                lhsT_scale=weights[1][:, c0 : c0 + P],
                rhs=words[:, w0 : w0 + width].bitcast(FP8X4),
                rhs_scale=picked_scales[:, e0 : e0 + width],
                start=start,
                stop=stop,
            )

        def bank(name, tag=None):
            return psum.tile([P, G], F32, name=name, tag=tag or name)

        def half(tile, h):
            return tile[:, h * W : (h + 1) * W]

        d_head = bank("d_head")
        d_tail = [bank("d_tail0"), bank("d_tail1")]
        base_held = bank("base_held")

        gate = keep.tile([P, 6 * W], F32, name="gate")
        prod = keep.tile([P, 6 * W], F32, name="prod")
        res = keep.tile([P, 6 * W], F32, name="res")
        held = keep.tile([P, 6 * W], F32, name="held")

        def tanh_half(piece, src):
            nc.scalar.activation(out=half(gate, piece), in_=src, func=ACT.Tanh, scale=-0.5)

        def hold(piece, src):
            nc.scalar.activation(out=half(held, piece), in_=src, func=ACT.Copy, scale=2.0)

        def weigh(dst, piece, shift, src, cols=slice(0, W)):
            nc.vector.scalar_tensor_tensor(
                out=half(dst, piece)[:, cols],
                in0=half(gate, piece)[:, cols],
                scalar=shift,
                in1=src[:, cols],
                op0=ALU.add,
                op1=ALU.mult,
            )

        def join_held(piece):
            nc.gpsimd.tensor_tensor(out=half(res, piece), in0=half(held, piece), in1=half(prod, piece), op=ALU.subtract)

        def join_base(piece, src, cols=slice(0, W)):
            nc.vector.scalar_tensor_tensor(
                out=half(res, piece)[:, cols],
                in0=src[:, cols],
                scalar=2.0,
                in1=half(prod, piece)[:, cols],
                op0=ALU.mult,
                op1=ALU.subtract,
            )

        def store_tail(queue, m, v0, v1):
            c0 = 2 * W + m * G - W
            queue.dma_start(out=out[m * P : (m + 1) * P, v0:v1], in_=res[:, c0 + v0 : c0 + v1])

        warm = bank("warm", "f_tail1")
        for rep in range(WARM):
            nc.tensor.matmul_mx(
                out=warm[0:32, :],
                lhsT=w1q[0][:, 0:32].bitcast(FP8X4),
                lhsT_scale=w1q[1][:, 0:32],
                rhs=w1q[0][:].bitcast(FP8X4),
                rhs_scale=w1q[1][:],
                start=True,
                stop=True,
            )

        gather_words(early[:, 0:G], 0)
        for m in range(2):
            mm(half(d_head, m), w1q, m * P, early, 0, W, m == 0, False)
        for m in range(2):
            mm(half(d_tail[m], 0), w1q, m * P, early, W, W, True, False)

        gather_words(early[:, G : 2 * G], G)
        for m in range(2):
            mm(half(d_head, m), w1q, N + m * P, early, V, W, False, m == 1)
        tanh_half(1, half(d_head, 1))
        cast(minus_staged[1][:], w2_raw[:, :, P:N], -0.5)
        tanh_half(0, half(d_head, 0))
        for m in range(2):
            mm(half(d_tail[m], 1), w1q, m * P, early, G, W, False, False)

        plus = quantise("plus", plus_staged, N)
        h_head0 = bank("h_head0")
        mm(half(h_head0, 0), plus, P, early, 0, W, True, True)
        mm(half(h_head0, 1), plus, P, early, V, W, True, True)
        f_head1 = bank("f_head1")
        mm(half(f_head1, 0), plus, 0, early, 0, W, True, False)
        mm(half(f_head1, 1), plus, 0, early, 0, W, False, False)
        f_tail = [bank("f_tail0"), bank("f_tail1")]
        mm(f_tail[0][:], plus, 0, early, W, G, True, False)

        late = shared.tile([P, G], U32, name="late", align_bytes=256, offset=0)
        gather_words(late[:], 2 * G)
        minus = [quantise("minus0", minus_staged[0], P)]
        weigh(held, 1, 1.0, half(h_head0, 1))
        weigh(prod, 1, -1.0, half(h_head0, 0))
        join_held(1)
        minus.append(quantise("minus1", minus_staged[1], P))
        mm(d_tail[0][:], w1q, N, late, 2 * G, G, False, True)
        mm(half(f_head1, 0), minus[0], 0, early, V, W, False, True)
        mm(f_tail[0][:], minus[0], 0, late, 2 * G, G, False, True)
        mm(half(base_held, 0), plus, 0, early, W, W, True, True)
        mm(d_tail[1][:], w1q, N + P, late, 2 * G, G, False, True)
        mm(f_tail[1][:], plus, P, early, W, G, True, False)
        mm(f_tail[1][:], minus[1], 0, late, 2 * G, G, False, True)
        for piece in (2, 3):
            tanh_half(piece, half(d_tail[0], piece % 2))
        hold(2, half(base_held, 0))
        mm(half(base_held, 1), plus, P, early, W, W, True, True)
        base_end = bank("base_end", "d_head")
        for m in range(2):
            mm(half(base_end, m), plus, m * P, early, G, W, True, True)
        for piece in (4, 5):
            tanh_half(piece, half(d_tail[1], piece % 2))
        nc.scalar.activation(out=half(held, 4)[:, 0:P], in_=half(base_held, 1)[:, 0:P], func=ACT.Copy, scale=2.0)

        weigh(prod, 0, 1.0, half(f_head1, 0))
        weigh(prod, 2, 1.0, half(f_tail[0], 0))
        join_held(2)
        join_base(0, half(f_head1, 1))
        nc.sync.dma_start(
            out=out[:, 0:W].rearrange("(m p) v -> p m v", p=P),
            in_=res[:, 0 : 2 * W].rearrange("p (m v) -> p m v", m=2),
        )
        weigh(prod, 3, 1.0, half(f_tail[0], 1))
        weigh(prod, 4, 1.0, half(f_tail[1], 0))
        nc.gpsimd.tensor_tensor(
            out=half(res, 4)[:, 0:P], in0=half(held, 4)[:, 0:P], in1=half(prod, 4)[:, 0:P], op=ALU.subtract
        )
        join_base(3, half(base_end, 0))
        store_tail(nc.sync, 0, W, G)
        store_tail(nc.sync, 0, G, V)
        weigh(prod, 5, 1.0, half(f_tail[1], 1))
        join_base(4, half(base_held, 1), slice(P, W))
        store_tail(nc.sync, 1, W, G)
        join_base(5, half(base_end, 1))
        store_tail(nc.scalar, 1, G, V)
